import numpy as np
import ml_dtypes


def mxq(x, axis, fmt="e4m3"):
    dtype, down = {"e4m3": (ml_dtypes.float8_e4m3fn, 7), "e5m2": (ml_dtypes.float8_e5m2, 14)}[fmt]
    v = np.moveaxis(np.asarray(x, np.float32).astype(ml_dtypes.bfloat16).astype(np.float64), axis, -1)
    blocks = v.reshape(v.shape[:-1] + (-1, 32))
    amax = np.abs(blocks).max(-1, keepdims=True)
    byte = np.maximum(np.where(amax > 0, np.frexp(amax)[1] - 1 + 127, 0) - down, 1)
    scale = np.exp2(byte - 127.0)
    codes = (blocks / scale).astype(np.float32).astype(dtype).astype(np.float64)
    return np.moveaxis((codes * scale).reshape(v.shape), -1, axis)


WIDE = False


def mx_kscale(k):
    if not WIDE:
        return np.ones(k)
    levels = np.array([10, -10, 5, -5, 0])
    if k % 512:
        return np.exp2(np.random.permutation(np.resize(levels, k // 32))).repeat(32)
    a = np.empty((k // 512, 16))
    for p in range(k // 512):
        a[p, :8] = np.random.permutation(np.resize(levels, 8))
        for g in range(8):
            far = levels[np.abs(levels - a[p, g]) >= 10]
            a[p, g + 8] = far[np.random.randint(len(far))]
    return np.exp2(a.ravel()).repeat(32)


BF16 = ml_dtypes.bfloat16


def bf(x):
    return np.asarray(x, np.float32).astype(BF16)


def f64(x):
    return np.asarray(x).astype(np.float64)


N, K, M = 1024, 1024, 512
RADIUS = 64.0


def smoothed_vertex(grad):
    v = -2.0 * grad
    ex = np.exp(v - v.max(-1, keepdims=True))
    return RADIUS * (ex / ex.sum(-1, keepdims=True))


def draw0():
    s, t = mx_kscale(M), mx_kscale(K)
    r = bf(0.5 * np.random.standard_normal((N, M)))
    p = 1.0 + 0.1 * np.random.standard_normal(M)
    enc = np.random.standard_normal((M, K)) * 2.0 / np.sqrt(M)
    g = 1.0 + 0.1 * np.random.standard_normal(K)
    dec = np.random.standard_normal((K, M)) * 0.045 * (K / M) ** 0.25
    grad = (f64(r) * p[None, :]) @ enc
    far = np.random.uniform(size=(N, 1)) < 0.125
    z = np.where(far, 400.0 / K * np.maximum(-grad, 0.0), np.random.uniform(0.0, 2.0 * RADIUS / K, (N, K)))
    return {"r": r, "z": bf(z), "p": bf(p * s), "enc": bf(enc / s[:, None]), "g": bf(g * t), "dec": bf(dec / t[:, None])}


def core(r, z, p, enc, g, dec):
    m, k = enc.shape
    r, z, p, g = f64(r), f64(z), f64(p), f64(g)
    grad = mxq(r * p[None, :], 1, "e4m3") @ mxq(f64(enc), 0, "e4m3")
    s = smoothed_vertex(grad)
    d = s - z
    e = mxq(d * g[None, :], 1, "e4m3") @ mxq(f64(dec), 0, "e4m3")
    gap = -np.sum(grad * d, axis=-1) / np.sqrt(m * k)
    curv = np.mean(e * e, axis=-1) + 1e-6
    gamma = np.minimum(np.maximum(gap / curv, 0.0), 1.0)
    return r + gamma[:, None] * e


def e4m3fn_bytes(y):
    return np.clip(np.asarray(y, np.float64), -448.0, 448.0).astype(np.float32).astype(ml_dtypes.float8_e4m3fn).view(np.uint8)


def e4m3fn_values(b):
    return np.asarray(b, np.uint8).view(ml_dtypes.float8_e4m3fn).astype(np.float64)


def setup_inputs():
    d = draw0()
    x0 = np.asarray(d['enc']).astype(np.float64)
    s = (np.max(np.abs(x0), axis=(1,), keepdims=True) / 448.0).astype(np.float32)
    out = {}
    for k, v in d.items():
        if k == 'enc':
            out['enc_bytes'] = e4m3fn_bytes(x0 / s.astype(np.float64))
            out['enc_scale'] = s
        else:
            out[k] = v
    return out


def reference(r, z, p, enc_bytes, enc_scale, g, dec):
    return core(r, z, p, e4m3fn_values(enc_bytes) * enc_scale.astype(np.float64), g, dec)

@@ -1,0 +1,395 @@
+import math
+from contextlib import ExitStack
+
+import concourse.mybir as mybir
+from concourse.masks import make_identity
+
+F32 = mybir.dt.float32
+BF16 = mybir.dt.bfloat16
+U32 = mybir.dt.uint32
+U8 = mybir.dt.uint8
+FP8 = mybir.dt.float8_e4m3fn
+FP8X4 = mybir.dt.float8_e4m3fn_x4
+ALU = mybir.AluOpType
+ACT = mybir.ActivationFunctionType
+AX = mybir.AxisListType
+
+N, K, M = 1024, 1024, 512
+P = 128
+TILES = N // P
+HALF = 512
+PASSES = K // HALF
+RADIUS = 64.0
+
+FLOPS = 2 * 2 * N * K * M
+
+S_PLANES = (2, 1)
+V_COLS = (256, 320)
+
+
+def tile_smoothedfrankwolfesimplexcoding_kernel(tc, r, z, p, enc_bytes, enc_scale, g, dec, out):
+    nc = tc.nc
+    gap_factor = -1.0 / math.sqrt(M * K)
+    mean_root = 1.0 / math.sqrt(M)
+
+    r_rows = r.rearrange("(q j) k -> q j k", j=TILES)
+    z_rows = z.rearrange("(q j) k -> q j k", j=TILES)
+    out_rows = out.rearrange("(q j) m -> q j m", j=TILES)
+    enc_rows = enc_bytes.rearrange("(q t) n -> q t n", t=4)
+    dec_rows = dec.rearrange("(h q t) m -> h q t m", q=P, t=4)
+
+    with ExitStack() as ctx:
+        keep = ctx.enter_context(tc.tile_pool(name="keep", bufs=1))
+        work = ctx.enter_context(tc.tile_pool(name="work", bufs=2))
+        stat = ctx.enter_context(tc.tile_pool(name="stat", bufs=4))
+        psum = ctx.enter_context(tc.psum_pool(name="psum", bufs=2))
+        ctx.enter_context(tc.manual_schedule())
+
+        scale_t = keep.tile([P, 4], F32, name="scale_t")
+        p_t = keep.tile([P, 4], BF16, name="p_t")
+        enc_raw = [keep.tile([P, 4, HALF], U8, name="enc_raw%d" % h) for h in range(2)]
+        r_t = [keep.tile([P, 2, M], BF16, name="r_t%d" % m) for m in range(TILES // 2)]
+        z_t = [keep.tile([P, K], BF16, name="z_t%d" % j) for j in range(TILES)]
+        g_t = keep.tile([P, K], BF16, name="g_t")
+        dec_raw = [keep.tile([P, 4, M], BF16, name="dec_raw%d" % h) for h in range(PASSES)]
+
+        nc.scalar.dma_start(out=scale_t[:], in_=enc_scale.rearrange("(q t) o -> q (t o)", t=4))
+        nc.scalar.dma_start(out=p_t[:], in_=p.rearrange("(q t) -> q t", t=4))
+        nc.sync.dma_start(out=enc_raw[0][:], in_=enc_rows[:, :, 0:HALF])
+        nc.sync.dma_start(out=r_t[0][:], in_=r_rows[:, 0:2, :])
+        nc.sync.dma_start(out=enc_raw[1][:], in_=enc_rows[:, :, HALF:K])
+        nc.sync.dma_start(out=dec_raw[0][:], in_=dec_rows[0])
+        nc.sync.dma_start(out=r_t[1][:], in_=r_rows[:, 2:4, :])
+        nc.sync.dma_start(out=z_t[0][:], in_=z_rows[:, 0, :])
+        nc.sync.dma_start(out=dec_raw[1][:], in_=dec_rows[1])
+        nc.sync.dma_start(out=g_t[:], in_=g.partition_broadcast(P))
+        nc.sync.dma_start(out=z_t[1][:], in_=z_rows[:, 1, :])
+        nc.sync.dma_start(out=r_t[2][:], in_=r_rows[:, 4:6, :])
+        nc.sync.dma_start(out=z_t[2][:], in_=z_rows[:, 2, :])
+        nc.sync.dma_start(out=r_t[3][:], in_=r_rows[:, 6:8, :])
+        for j in range(3, TILES):
+            nc.sync.dma_start(out=z_t[j][:], in_=z_rows[:, j, :])
+
+        ident = keep.tile([P, P], F32, name="ident")
+        warm = keep.tile([P, 1], F32, name="warm")
+        nc.vector.memset(warm[:], 0.0)
+        nc.scalar.activation(out=warm[:], in_=warm[:], func=ACT.Exp)
+        make_identity(nc, ident[:])
+
+        enc_plane = [keep.tile([P, 4, HALF], BF16, name="enc_plane%d" % h) for h in range(2)]
+        enc_group = [keep.tile([P, HALF, 4], BF16, name="enc_group%d" % h, align_bytes=64) for h in range(2)]
+        enc_codes = keep.tile([P, K], U32, name="enc_codes", align_bytes=64)
+        enc_scales = keep.tile([P, K], U8, name="enc_scales", align_bytes=64)
+        dec_group = [keep.tile([P, M, 4], BF16, name="dec_group%d" % h, align_bytes=64) for h in range(PASSES)]
+        dec_codes = keep.tile([P, PASSES, M], U32, name="dec_codes", align_bytes=64)
+        dec_scales = keep.tile([P, PASSES, M], U8, name="dec_scales", align_bytes=64)
+        rp_codes = [keep.tile([P, 2 * P], U32, name="rp_codes%d" % m, align_bytes=64) for m in range(TILES // 2)]
+        rp_scales = [keep.tile([P, 2 * P], U8, name="rp_scales%d" % m, align_bytes=64) for m in range(TILES // 2)]
+
+        def enc_widen(h):
+            for t in range(4):
+                src = enc_raw[h][:, t, :].bitcast(FP8)
+                dst = enc_plane[h][:, t, :]
+                if t < S_PLANES[h]:
+                    nc.scalar.activation(out=dst, in_=src, func=ACT.Copy, scale=scale_t[:, t : t + 1])
+                else:
+                    nc.vector.tensor_scalar(
+                        out=dst, in0=src, scalar1=scale_t[:, t : t + 1], scalar2=None, op0=ALU.mult
+                    )
+
+        def enc_interleave(h):
+            c = V_COLS[h]
+            nc.vector.tensor_copy(
+                out=enc_group[h][:, 0:c, :], in_=enc_plane[h][:, :, 0:c].rearrange("q t n -> q n t")
+            )
+            nc.scalar.copy(
+                out=enc_group[h][:, c:HALF, :], in_=enc_plane[h][:, :, c:HALF].rearrange("q t n -> q n t")
+            )
+
+        def enc_quantize(h):
+            cols = slice(h * HALF, (h + 1) * HALF)
+            nc.vector.quantize_mx(
+                out=enc_codes[:, cols].bitcast(FP8X4),
+                scales=enc_scales[:, cols],
+                in_=enc_group[h][:].rearrange("q n t -> q (n t)"),
+            )
+
+        def dec_interleave(h):
+            nc.scalar.copy(out=dec_group[h][:], in_=dec_raw[h][:].rearrange("q t n -> q n t"))
+
+        def dec_quantize(h):
+            nc.vector.quantize_mx(
+                out=dec_codes[:, h, :].bitcast(FP8X4),
+                scales=dec_scales[:, h, :],
+                in_=dec_group[h][:].rearrange("q n t -> q (n t)"),
+            )
+
+        rt = {}
+        rp = {}
+
+        def r_transpose(m):
+            rt[m] = psum.tile([P, 2, 2 * P], F32, name="rt%d" % m, tag="turn")
+            for j in range(2):
+                words = r_t[m][:, j, :].bitcast(F32)
+                for u in range(2):
+                    nc.tensor.transpose(rt[m][:, u, j * P : (j + 1) * P], words[:, u::2], ident[:])
+
+        def r_gain(m):
+            rp[m] = work.tile([P, 2 * P, 4], BF16, name="rp%d" % m, tag="rp", align_bytes=64)
+            nc.vector.tensor_tensor(
+                out=rp[m][:].rearrange("q i (u e) -> q i u e", u=2),
+                in0=rt[m][:].rearrange("q u i -> q (u i)").bitcast(BF16).rearrange("q (u i e) -> q i u e", u=2, e=2),
+                in1=p_t[:].rearrange("q (u e) -> q u e", u=2).unsqueeze(1).to_broadcast([P, 2 * P, 2, 2]),
+                op=ALU.mult,
+            )
+
+        def r_quantize(m):
+            nc.vector.quantize_mx(
+                out=rp_codes[m][:].bitcast(FP8X4),
+                scales=rp_scales[m][:],
+                in_=rp[m][:].rearrange("q i t -> q (i t)"),
+            )
+
+        grad = {}
+        mins = {}
+        bias = {}
+        ex = {}
+        sums = {}
+        coef = {}
+        d = {}
+        dg = {}
+        gaps = {}
+        turned = {}
+        dgt = {}
+        dq = {}
+        e = {}
+        curv = {}
+        gamma = {}
+
+        def grad_matmul(i, h):
+            if h == 0:
+                grad[i] = [None, None]
+            bank = psum.tile([P, HALF], F32, name="grad%d_%d" % (i, h), tag="grad%d" % h)
+            grad[i][h] = bank
+            rows = slice((i % 2) * P, (i % 2 + 1) * P)
+            cols = slice(h * HALF, (h + 1) * HALF)
+            nc.tensor.matmul_mx(
+                out=bank[:],
+                lhsT=rp_codes[i // 2][:, rows].bitcast(FP8X4),
+                lhsT_scale=rp_scales[i // 2][:, rows],
+                rhs=enc_codes[:, cols].bitcast(FP8X4),
+                rhs_scale=enc_scales[:, cols],
+                start=True,
+                stop=True,
+            )
+
+        def grad_min(i, h):
+            if h == 0:
+                mins[i] = stat.tile([P, 2], F32, name="mins%d" % i, tag="mins")
+            nc.vector.tensor_reduce(out=mins[i][:, h : h + 1], in_=grad[i][h][:], axis=AX.X, op=ALU.min)
+
+        def exp_bias(i):
+            bias[i] = stat.tile([P, 1], F32, name="bias%d" % i, tag="bias")
+            nc.vector.tensor_scalar(
+                out=bias[i][:], in0=mins[i][:, 0:1], scalar1=mins[i][:, 1:2], scalar2=2.0, op0=ALU.min, op1=ALU.mult
+            )
+
+        def exps(i):
+            ex[i] = work.tile([P, K], F32, name="ex%d" % i, tag="ex")
+            sums[i] = stat.tile([P, 2], F32, name="sums%d" % i, tag="sums")
+            for h in range(2):
+                nc.scalar.activation(
+                    out=ex[i][:, h * HALF : (h + 1) * HALF],
+                    in_=grad[i][h][:],
+                    func=ACT.Exp,
+                    scale=-2.0,
+                    bias=bias[i][:],
+                    accum_out=sums[i][:, h : h + 1],
+                )
+
+        def coef_a(i):
+            coef[i] = stat.tile([P, 2], F32, name="coef%d" % i, tag="coef")
+            nc.vector.tensor_scalar(
+                out=coef[i][:, 0:1],
+                in0=sums[i][:, 0:1],
+                scalar1=sums[i][:, 1:2],
+                scalar2=1.0 / RADIUS,
+                op0=ALU.add,
+                op1=ALU.mult,
+            )
+
+        def coef_b(i):
+            nc.vector.reciprocal(out=coef[i][:, 1:2], in_=coef[i][:, 0:1])
+
+        def direction(i):
+            d[i] = work.tile([P, K], F32, name="d%d" % i, tag="d")
+            nc.vector.scalar_tensor_tensor(
+                out=d[i][:], in0=ex[i][:], scalar=coef[i][:, 1:2], in1=z_t[i][:], op0=ALU.mult, op1=ALU.subtract
+            )
+
+        def gained(i):
+            dg[i] = work.tile([P, K], BF16, name="dg%d" % i, tag="dg")
+            for h in range(2):
+                cols = slice(h * HALF, (h + 1) * HALF)
+                nc.gpsimd.tensor_tensor(out=dg[i][:, cols], in0=d[i][:, cols], in1=g_t[:, cols], op=ALU.mult)
+
+        def gap_sum(i, h):
+            if h == 0:
+                gaps[i] = stat.tile([P, 2], F32, name="gaps%d" % i, tag="gaps")
+            junk = work.tile([P, HALF], F32, name="junk%d_%d" % (i, h), tag="junk")
+            nc.vector.scalar_tensor_tensor(
+                out=junk[:],
+                in0=grad[i][h][:],
+                scalar=gap_factor,
+                in1=d[i][:, h * HALF : (h + 1) * HALF],
+                op0=ALU.mult,
+                op1=ALU.mult,
+                accum_out=gaps[i][:, h : h + 1],
+            )
+
+        def dg_transpose(i):
+            turned[i] = psum.tile([P, 2, 2, P], F32, name="turned%d" % i, tag="turn")
+            words = dg[i][:].bitcast(F32)
+            for h in range(2):
+                for u in range(2):
+                    nc.tensor.transpose(turned[i][:, h, u, :], words[:, 256 * h + u : 256 * (h + 1) : 2], ident[:])
+
+        def dg_copy(i):
+            dgt[i] = work.tile([P, 2, P, 4], BF16, name="dgt%d" % i, tag="dgt", align_bytes=64)
+            nc.scalar.copy(
+                out=dgt[i][:].rearrange("q h i t -> q (h i t)").bitcast(F32).rearrange("q (h i u) -> q h i u", h=2, u=2),
+                in_=turned[i][:].rearrange("q h u i -> q h i u"),
+            )
+
+        def dg_quantize(i):
+            codes = work.tile([P, 2 * P], U32, name="dq_codes%d" % i, tag="dq_codes", align_bytes=64)
+            scales = work.tile([P, 2 * P], U8, name="dq_scales%d" % i, tag="dq_scales", align_bytes=64)
+            dq[i] = (codes, scales)
+            nc.vector.quantize_mx(
+                out=codes[:].bitcast(FP8X4), scales=scales[:], in_=dgt[i][:].rearrange("q h i t -> q (h i t)")
+            )
+
+        def e_matmul(i):
+            bank = psum.tile([P, M], F32, name="e%d" % i, tag="e")
+            e[i] = bank
+            codes, scales = dq[i]
+            for h in range(PASSES):
+                nc.tensor.matmul_mx(
+                    out=bank[:],
+                    lhsT=codes[:, h * P : (h + 1) * P].bitcast(FP8X4),
+                    lhsT_scale=scales[:, h * P : (h + 1) * P],
+                    rhs=dec_codes[:, h, :].bitcast(FP8X4),
+                    rhs_scale=dec_scales[:, h, :],
+                    start=(h == 0),
+                    stop=(h == PASSES - 1),
+                )
+
+        def curvature(i):
+            curv[i] = stat.tile([P, 3], F32, name="curv%d" % i, tag="curv")
+            square = work.tile([P, M], F32, name="square%d" % i, tag="square")
+            nc.scalar.activation(
+                out=square[:], in_=e[i][:], func=ACT.Square, scale=mean_root, accum_out=curv[i][:, 0:1]
+            )
+            nc.scalar.activation(out=curv[i][:, 1:2], in_=curv[i][:, 0:1], func=ACT.Copy, bias=1e-6)
+
+        def gamma_a(i):
+            gamma[i] = stat.tile([P, 3], F32, name="gamma%d" % i, tag="gamma")
+            nc.vector.reciprocal(out=gamma[i][:, 0:1], in_=curv[i][:, 1:2])
+
+        def gamma_b(i):
+            nc.vector.tensor_scalar(
+                out=gamma[i][:, 1:2],
+                in0=gaps[i][:, 0:1],
+                scalar1=gaps[i][:, 1:2],
+                scalar2=gamma[i][:, 0:1],
+                op0=ALU.add,
+                op1=ALU.mult,
+            )
+
+        def gamma_c(i):
+            nc.vector.tensor_scalar(
+                out=gamma[i][:, 2:3], in0=gamma[i][:, 1:2], scalar1=0.0, scalar2=1.0, op0=ALU.max, op1=ALU.min
+            )
+
+        def update(i):
+            res = work.tile([P, M], F32, name="res%d" % i, tag="res")
+            nc.vector.scalar_tensor_tensor(
+                out=res[:],
+                in0=e[i][:],
+                scalar=gamma[i][:, 2:3],
+                in1=r_t[i // 2][:, i % 2, :],
+                op0=ALU.mult,
+                op1=ALU.add,
+            )
+            nc.sync.dma_start(out=out_rows[:, i, :], in_=res[:])
+
+        r_transpose(0)
+        enc_widen(0)
+        enc_interleave(0)
+        r_gain(0)
+        enc_quantize(0)
+        r_quantize(0)
+        grad_matmul(0, 0)
+        r_transpose(1)
+        enc_widen(1)
+        enc_interleave(1)
+        grad_min(0, 0)
+        enc_quantize(1)
+        grad_matmul(0, 1)
+        grad_matmul(1, 0)
+        grad_matmul(1, 1)
+        dec_interleave(0)
+        grad_min(0, 1)
+        r_gain(1)
+        exp_bias(0)
+        exps(0)
+        dec_interleave(1)
+        r_quantize(1)
+        dec_quantize(0)
+        coef_a(0)
+        coef_b(0)
+
+        last = TILES - 1
+        for i in range(TILES + 2):
+            if i < TILES:
+                direction(i)
+                gained(i)
+            if 0 <= i - 2:
+                gamma_c(i - 2)
+            if i < last:
+                grad_min(i + 1, 0)
+                grad_min(i + 1, 1)
+            if 0 <= i - 1 < TILES:
+                dg_quantize(i - 1)
+                e_matmul(i - 1)
+            if i < last:
+                exp_bias(i + 1)
+                exps(i + 1)
+            if 0 <= i - 1 < TILES:
+                curvature(i - 1)
+            if 0 <= i - 2:
+                update(i - 2)
+            if i < TILES:
+                gap_sum(i, 0)
+                gap_sum(i, 1)
+            if i == 0:
+                dec_quantize(1)
+            if i in (1, 3):
+                m = 2 + i // 2
+                r_transpose(m)
+                r_gain(m)
+                r_quantize(m)
+            if i + 2 < TILES:
+                grad_matmul(i + 2, 0)
+                grad_matmul(i + 2, 1)
+            if i < TILES:
+                dg_transpose(i)
+                dg_copy(i)
+            if i < last:
+                coef_a(i + 1)
+            if 0 <= i - 1 < TILES:
+                gamma_a(i - 1)
+            if i < last:
+                coef_b(i + 1)
+            if 0 <= i - 1 < TILES:
+                gamma_b(i - 1)

@@ -23,8 +23,14 @@ RADIUS = 64.0
 
 FLOPS = 2 * 2 * N * K * M
 
-S_PLANES = (2, 1)
-V_COLS = (256, 320)
+CHUNK = 256
+CHUNKS = K // CHUNK
+S_PLANES = (2, 3, 3, 3)
+HEAD = [("rT", 0), ("W", 1), ("W", 2), ("rG", 0), ("W", 3), ("W", 0), ("I128", 3), ("I", 2), ("I", 0), ("I", 1), ("rQ", 0), ("EQ", 0), ("EQ", 1), ("G0", 0), ("EQ", 3), ("EQ", 2), ("G1", 0), ("DI", 1), ("DQ", 1), ("m0", 0), ("rT", 1), ("DI", 0), ("m1", 0), ("b", 0), ("rT", 2), ("G0", 1), ("rG", 1), ("rG", 2), ("DQ", 0), ("G1", 1), ("x0", 0), ("x1", 0), ("xs", 0), ("rQ", 2), ("c", 0), ("rQ", 1)]
+LOOP = [("m0", 1), ("m1", 1), ("C", 0), ("b", 1), ("rQ", 3), ("q", -1), ("E", -1), ("x0", 1), ("x1", 1), ("D0", 0), ("G0", 2), ("xs", 1), ("G1", 2), ("s", -1), ("u", -3), ("g0", 0), ("g1", 0), ("r", -2), ("D1", 0), ("rG", 4), ("rT", 5), ("T", 0), ("rl", 0), ("c", 1), ("y", 0), ("k", -2)]
+TAIL = [("q", 5), ("k", 4), ("C2", 7), ("u", 4), ("E", 5), ("V0", 7), ("V1", 7), ("s", 5), ("r", 5), ("q", 6), ("k", 5), ("T0", 7), ("g0", 7), ("T1", 7), ("y0", 7), ("y1", 7), ("E", 6), ("u", 5), ("q0", 7), ("s", 6), ("q1", 7), ("E", 7), ("s", 7), ("g1", 7), ("r", 6), ("k", 6), ("u", 6), ("rl", 7), ("r", 7), ("k", 7), ("u2", 7)]
+STEPS = 7
+SPECIAL = (7,)
 
 
 def tile_smoothedfrankwolfesimplexcoding_kernel(tc, r, z, p, enc_bytes, enc_scale, g, dec, out):
@@ -41,7 +47,7 @@ def tile_smoothedfrankwolfesimplexcoding_kernel(tc, r, z, p, enc_bytes, enc_scal
     with ExitStack() as ctx:
         keep = ctx.enter_context(tc.tile_pool(name="keep", bufs=1))
         work = ctx.enter_context(tc.tile_pool(name="work", bufs=2))
-        stat = ctx.enter_context(tc.tile_pool(name="stat", bufs=4))
+        stat = ctx.enter_context(tc.tile_pool(name="stat", bufs=6))
         psum = ctx.enter_context(tc.psum_pool(name="psum", bufs=2))
         ctx.enter_context(tc.manual_schedule())
 
@@ -76,8 +82,8 @@ def tile_smoothedfrankwolfesimplexcoding_kernel(tc, r, z, p, enc_bytes, enc_scal
         nc.scalar.activation(out=warm[:], in_=warm[:], func=ACT.Exp)
         make_identity(nc, ident[:])
 
-        enc_plane = [keep.tile([P, 4, HALF], BF16, name="enc_plane%d" % h) for h in range(2)]
-        enc_group = [keep.tile([P, HALF, 4], BF16, name="enc_group%d" % h, align_bytes=64) for h in range(2)]
+        enc_plane = [keep.tile([P, 4, CHUNK], BF16, name="enc_plane%d" % c) for c in range(CHUNKS)]
+        enc_group = [keep.tile([P, CHUNK, 4], BF16, name="enc_group%d" % c, align_bytes=64) for c in range(CHUNKS)]
         enc_codes = keep.tile([P, K], U32, name="enc_codes", align_bytes=64)
         enc_scales = keep.tile([P, K], U8, name="enc_scales", align_bytes=64)
         dec_group = [keep.tile([P, M, 4], BF16, name="dec_group%d" % h, align_bytes=64) for h in range(PASSES)]
@@ -86,32 +92,30 @@ def tile_smoothedfrankwolfesimplexcoding_kernel(tc, r, z, p, enc_bytes, enc_scal
         rp_codes = [keep.tile([P, 2 * P], U32, name="rp_codes%d" % m, align_bytes=64) for m in range(TILES // 2)]
         rp_scales = [keep.tile([P, 2 * P], U8, name="rp_scales%d" % m, align_bytes=64) for m in range(TILES // 2)]
 
-        def enc_widen(h):
+        def enc_widen(c):
+            first = c * CHUNK % HALF
             for t in range(4):
-                src = enc_raw[h][:, t, :].bitcast(FP8)
-                dst = enc_plane[h][:, t, :]
-                if t < S_PLANES[h]:
+                src = enc_raw[c * CHUNK // HALF][:, t, first : first + CHUNK].bitcast(FP8)
+                dst = enc_plane[c][:, t, :]
+                if t < S_PLANES[c]:
                     nc.scalar.activation(out=dst, in_=src, func=ACT.Copy, scale=scale_t[:, t : t + 1])
                 else:
                     nc.vector.tensor_scalar(
                         out=dst, in0=src, scalar1=scale_t[:, t : t + 1], scalar2=None, op0=ALU.mult
                     )
 
-        def enc_interleave(h):
-            c = V_COLS[h]
-            nc.vector.tensor_copy(
-                out=enc_group[h][:, 0:c, :], in_=enc_plane[h][:, :, 0:c].rearrange("q t n -> q n t")
-            )
-            nc.scalar.copy(
-                out=enc_group[h][:, c:HALF, :], in_=enc_plane[h][:, :, c:HALF].rearrange("q t n -> q n t")
-            )
+        def enc_interleave(c, s=0):
+            n = CHUNK - s
+            nc.vector.tensor_copy(out=enc_group[c][:, 0:n, :], in_=enc_plane[c][:, :, 0:n].rearrange("q t n -> q n t"))
+            if s:
+                nc.scalar.copy(out=enc_group[c][:, n:CHUNK, :], in_=enc_plane[c][:, :, n:CHUNK].rearrange("q t n -> q n t"))
 
-        def enc_quantize(h):
-            cols = slice(h * HALF, (h + 1) * HALF)
+        def enc_quantize(c):
+            cols = slice(c * CHUNK, (c + 1) * CHUNK)
             nc.vector.quantize_mx(
                 out=enc_codes[:, cols].bitcast(FP8X4),
                 scales=enc_scales[:, cols],
-                in_=enc_group[h][:].rearrange("q n t -> q (n t)"),
+                in_=enc_group[c][:].rearrange("q n t -> q (n t)"),
             )
 
         def dec_interleave(h):
@@ -165,16 +169,16 @@ def tile_smoothedfrankwolfesimplexcoding_kernel(tc, r, z, p, enc_bytes, enc_scal
         e = {}
         curv = {}
         gamma = {}
+        step = {}
+        tot = {}
+        pos = {}
 
         def grad_matmul(i, h):
-            if h == 0:
-                grad[i] = [None, None]
-            bank = psum.tile([P, HALF], F32, name="grad%d_%d" % (i, h), tag="grad%d" % h)
-            grad[i][h] = bank
+            grad[i, h] = psum.tile([P, HALF], F32, name="grad%d_%d" % (i, h), tag="grad%d" % h)
             rows = slice((i % 2) * P, (i % 2 + 1) * P)
             cols = slice(h * HALF, (h + 1) * HALF)
             nc.tensor.matmul_mx(
-                out=bank[:],
+                out=grad[i, h][:],
                 lhsT=rp_codes[i // 2][:, rows].bitcast(FP8X4),
                 lhsT_scale=rp_scales[i // 2][:, rows],
                 rhs=enc_codes[:, cols].bitcast(FP8X4),
@@ -186,7 +190,7 @@ def tile_smoothedfrankwolfesimplexcoding_kernel(tc, r, z, p, enc_bytes, enc_scal
         def grad_min(i, h):
             if h == 0:
                 mins[i] = stat.tile([P, 2], F32, name="mins%d" % i, tag="mins")
-            nc.vector.tensor_reduce(out=mins[i][:, h : h + 1], in_=grad[i][h][:], axis=AX.X, op=ALU.min)
+            nc.vector.tensor_reduce(out=mins[i][:, h : h + 1], in_=grad[i, h][:], axis=AX.X, op=ALU.min)
 
         def exp_bias(i):
             bias[i] = stat.tile([P, 1], F32, name="bias%d" % i, tag="bias")
@@ -194,44 +198,49 @@ def tile_smoothedfrankwolfesimplexcoding_kernel(tc, r, z, p, enc_bytes, enc_scal
                 out=bias[i][:], in0=mins[i][:, 0:1], scalar1=mins[i][:, 1:2], scalar2=2.0, op0=ALU.min, op1=ALU.mult
             )
 
-        def exps(i):
-            ex[i] = work.tile([P, K], F32, name="ex%d" % i, tag="ex")
-            sums[i] = stat.tile([P, 2], F32, name="sums%d" % i, tag="sums")
-            for h in range(2):
-                nc.scalar.activation(
-                    out=ex[i][:, h * HALF : (h + 1) * HALF],
-                    in_=grad[i][h][:],
-                    func=ACT.Exp,
-                    scale=-2.0,
-                    bias=bias[i][:],
-                    accum_out=sums[i][:, h : h + 1],
-                )
+        def exp_half(i, h):
+            if h == 0:
+                ex[i] = work.tile([P, K], F32, name="ex%d" % i, tag="ex")
+                sums[i] = stat.tile([P, 2], F32, name="sums%d" % i, tag="sums")
+            nc.scalar.activation(
+                out=ex[i][:, h * HALF : (h + 1) * HALF],
+                in_=grad[i, h][:],
+                func=ACT.Exp,
+                scale=-2.0,
+                bias=bias[i][:],
+                accum_out=sums[i][:, h : h + 1],
+            )
 
-        def coef_a(i):
-            coef[i] = stat.tile([P, 2], F32, name="coef%d" % i, tag="coef")
-            nc.vector.tensor_scalar(
-                out=coef[i][:, 0:1],
-                in0=sums[i][:, 0:1],
-                scalar1=sums[i][:, 1:2],
-                scalar2=1.0 / RADIUS,
-                op0=ALU.add,
-                op1=ALU.mult,
+        def exp_sum(i):
+            tot[i] = stat.tile([P, 2], F32, name="tot%d" % i, tag="tot")
+            nc.scalar.activation(out=tot[i][:, 0:1], in_=sums[i][:, 0:1], func=ACT.Copy, scale=1.0 / RADIUS)
+            nc.scalar.activation(
+                out=tot[i][:, 1:2], in_=sums[i][:, 1:2], func=ACT.Identity, scale=1.0 / RADIUS, bias=tot[i][:, 0:1]
             )
 
         def coef_b(i):
-            nc.vector.reciprocal(out=coef[i][:, 1:2], in_=coef[i][:, 0:1])
+            coef[i] = stat.tile([P, 1], F32, name="coef%d" % i, tag="coef")
+            nc.vector.reciprocal(out=coef[i][:], in_=tot[i][:, 1:2])
 
-        def direction(i):
+        def direction(i, parts=1):
             d[i] = work.tile([P, K], F32, name="d%d" % i, tag="d")
-            nc.vector.scalar_tensor_tensor(
-                out=d[i][:], in0=ex[i][:], scalar=coef[i][:, 1:2], in1=z_t[i][:], op0=ALU.mult, op1=ALU.subtract
-            )
+            w = K // parts
+            for h in range(parts):
+                cols = slice(h * w, (h + 1) * w)
+                nc.vector.scalar_tensor_tensor(
+                    out=d[i][:, cols],
+                    in0=ex[i][:, cols],
+                    scalar=coef[i][:],
+                    in1=z_t[i][:, cols],
+                    op0=ALU.mult,
+                    op1=ALU.subtract,
+                )
 
-        def gained(i):
-            dg[i] = work.tile([P, K], BF16, name="dg%d" % i, tag="dg")
-            for h in range(2):
-                cols = slice(h * HALF, (h + 1) * HALF)
-                nc.gpsimd.tensor_tensor(out=dg[i][:, cols], in0=d[i][:, cols], in1=g_t[:, cols], op=ALU.mult)
+        def gained(i, h, engine):
+            if h == 0:
+                dg[i] = work.tile([P, K], BF16, name="dg%d" % i, tag="dg")
+            cols = slice(h * HALF, (h + 1) * HALF)
+            engine.tensor_tensor(out=dg[i][:, cols], in0=d[i][:, cols], in1=g_t[:, cols], op=ALU.mult)
 
         def gap_sum(i, h):
             if h == 0:
@@ -239,7 +248,7 @@ def tile_smoothedfrankwolfesimplexcoding_kernel(tc, r, z, p, enc_bytes, enc_scal
             junk = work.tile([P, HALF], F32, name="junk%d_%d" % (i, h), tag="junk")
             nc.vector.scalar_tensor_tensor(
                 out=junk[:],
-                in0=grad[i][h][:],
+                in0=grad[i, h][:],
                 scalar=gap_factor,
                 in1=d[i][:, h * HALF : (h + 1) * HALF],
                 op0=ALU.mult,
@@ -247,26 +256,38 @@ def tile_smoothedfrankwolfesimplexcoding_kernel(tc, r, z, p, enc_bytes, enc_scal
                 accum_out=gaps[i][:, h : h + 1],
             )
 
-        def dg_transpose(i):
-            turned[i] = psum.tile([P, 2, 2, P], F32, name="turned%d" % i, tag="turn")
+        def dg_transpose(i, halves=(0, 1)):
+            if 0 in halves:
+                turned[i] = psum.tile([P, 2, 2, P], F32, name="turned%d" % i, tag="turn")
             words = dg[i][:].bitcast(F32)
-            for h in range(2):
+            for h in halves:
                 for u in range(2):
                     nc.tensor.transpose(turned[i][:, h, u, :], words[:, 256 * h + u : 256 * (h + 1) : 2], ident[:])
 
-        def dg_copy(i):
-            dgt[i] = work.tile([P, 2, P, 4], BF16, name="dgt%d" % i, tag="dgt", align_bytes=64)
+        def dg_copy(i, halves=(0, 1)):
+            if 0 in halves:
+                dgt[i] = work.tile([P, 2, P, 4], BF16, name="dgt%d" % i, tag="dgt", align_bytes=64)
+            h0, h1 = halves[0], halves[-1] + 1
             nc.scalar.copy(
-                out=dgt[i][:].rearrange("q h i t -> q (h i t)").bitcast(F32).rearrange("q (h i u) -> q h i u", h=2, u=2),
-                in_=turned[i][:].rearrange("q h u i -> q h i u"),
+                out=dgt[i][:]
+                .rearrange("q h i t -> q (h i t)")
+                .bitcast(F32)
+                .rearrange("q (h i u) -> q h i u", h=2, u=2)[:, h0:h1],
+                in_=turned[i][:].rearrange("q h u i -> q h i u")[:, h0:h1],
             )
 
-        def dg_quantize(i):
-            codes = work.tile([P, 2 * P], U32, name="dq_codes%d" % i, tag="dq_codes", align_bytes=64)
-            scales = work.tile([P, 2 * P], U8, name="dq_scales%d" % i, tag="dq_scales", align_bytes=64)
-            dq[i] = (codes, scales)
+        def dg_quantize(i, halves=(0, 1)):
+            if 0 in halves:
+                codes = work.tile([P, 2 * P], U32, name="dq_codes%d" % i, tag="dq_codes", align_bytes=64)
+                scales = work.tile([P, 2 * P], U8, name="dq_scales%d" % i, tag="dq_scales", align_bytes=64)
+                dq[i] = (codes, scales)
+            codes, scales = dq[i]
+            h0, h1 = halves[0], halves[-1] + 1
+            cols = slice(h0 * P, h1 * P)
             nc.vector.quantize_mx(
-                out=codes[:].bitcast(FP8X4), scales=scales[:], in_=dgt[i][:].rearrange("q h i t -> q (h i t)")
+                out=codes[:, cols].bitcast(FP8X4),
+                scales=scales[:, cols],
+                in_=dgt[i][:].rearrange("q h i t -> q (h i t)")[:, h0 * 4 * P : h1 * 4 * P],
             )
 
         def e_matmul(i):
@@ -292,104 +313,78 @@ def tile_smoothedfrankwolfesimplexcoding_kernel(tc, r, z, p, enc_bytes, enc_scal
             )
             nc.scalar.activation(out=curv[i][:, 1:2], in_=curv[i][:, 0:1], func=ACT.Copy, bias=1e-6)
 
-        def gamma_a(i):
-            gamma[i] = stat.tile([P, 3], F32, name="gamma%d" % i, tag="gamma")
-            nc.vector.reciprocal(out=gamma[i][:, 0:1], in_=curv[i][:, 1:2])
+        def gap_relu(i):
+            pos[i] = stat.tile([P, 1], F32, name="pos%d" % i, tag="pos")
+            nc.scalar.activation(out=pos[i][:], in_=gaps[i][:, 0:1], func=ACT.Relu, bias=gaps[i][:, 1:2])
 
-        def gamma_b(i):
-            nc.vector.tensor_scalar(
-                out=gamma[i][:, 1:2],
-                in0=gaps[i][:, 0:1],
-                scalar1=gaps[i][:, 1:2],
-                scalar2=gamma[i][:, 0:1],
-                op0=ALU.add,
-                op1=ALU.mult,
-            )
+        def gamma_a(i):
+            gamma[i] = stat.tile([P, 1], F32, name="gamma%d" % i, tag="gamma")
+            nc.vector.reciprocal(out=gamma[i][:], in_=curv[i][:, 1:2])
 
         def gamma_c(i):
+            step[i] = stat.tile([P, 1], F32, name="step%d" % i, tag="step")
             nc.vector.tensor_scalar(
-                out=gamma[i][:, 2:3], in0=gamma[i][:, 1:2], scalar1=0.0, scalar2=1.0, op0=ALU.max, op1=ALU.min
-            )
-
-        def update(i):
-            res = work.tile([P, M], F32, name="res%d" % i, tag="res")
-            nc.vector.scalar_tensor_tensor(
-                out=res[:],
-                in0=e[i][:],
-                scalar=gamma[i][:, 2:3],
-                in1=r_t[i // 2][:, i % 2, :],
+                out=step[i][:],
+                in0=pos[i][:],
+                scalar1=gamma[i][:],
+                scalar2=1.0,
                 op0=ALU.mult,
-                op1=ALU.add,
+                op1=ALU.min,
             )
-            nc.sync.dma_start(out=out_rows[:, i, :], in_=res[:])
 
-        r_transpose(0)
-        enc_widen(0)
-        enc_interleave(0)
-        r_gain(0)
-        enc_quantize(0)
-        r_quantize(0)
-        grad_matmul(0, 0)
-        r_transpose(1)
-        enc_widen(1)
-        enc_interleave(1)
-        grad_min(0, 0)
-        enc_quantize(1)
-        grad_matmul(0, 1)
-        grad_matmul(1, 0)
-        grad_matmul(1, 1)
-        dec_interleave(0)
-        grad_min(0, 1)
-        r_gain(1)
-        exp_bias(0)
-        exps(0)
-        dec_interleave(1)
-        r_quantize(1)
-        dec_quantize(0)
-        coef_a(0)
-        coef_b(0)
+        def update(i, parts=1):
+            res = work.tile([P, M], F32, name="res%d" % i, tag="res", bufs=4)
+            w = M // parts
+            for h in range(parts):
+                cols = slice(h * w, (h + 1) * w)
+                nc.vector.scalar_tensor_tensor(
+                    out=res[:, cols],
+                    in0=e[i][:, cols],
+                    scalar=step[i][:],
+                    in1=r_t[i // 2][:, i % 2, cols],
+                    op0=ALU.mult,
+                    op1=ALU.add,
+                )
+                nc.sync.dma_start(out=out_rows[:, i, cols], in_=res[:, cols])
 
-        last = TILES - 1
-        for i in range(TILES + 2):
-            if i < TILES:
-                direction(i)
-                gained(i)
-            if 0 <= i - 2:
-                gamma_c(i - 2)
-            if i < last:
-                grad_min(i + 1, 0)
-                grad_min(i + 1, 1)
-            if 0 <= i - 1 < TILES:
-                dg_quantize(i - 1)
-                e_matmul(i - 1)
-            if i < last:
-                exp_bias(i + 1)
-                exps(i + 1)
-            if 0 <= i - 1 < TILES:
-                curvature(i - 1)
-            if 0 <= i - 2:
-                update(i - 2)
-            if i < TILES:
-                gap_sum(i, 0)
-                gap_sum(i, 1)
-            if i == 0:
-                dec_quantize(1)
-            if i in (1, 3):
-                m = 2 + i // 2
-                r_transpose(m)
-                r_gain(m)
-                r_quantize(m)
-            if i + 2 < TILES:
-                grad_matmul(i + 2, 0)
-                grad_matmul(i + 2, 1)
-            if i < TILES:
-                dg_transpose(i)
-                dg_copy(i)
-            if i < last:
-                coef_a(i + 1)
-            if 0 <= i - 1 < TILES:
-                gamma_a(i - 1)
-            if i < last:
-                coef_b(i + 1)
-            if 0 <= i - 1 < TILES:
-                gamma_b(i - 1)
+        ops = {
+            "rT": r_transpose, "rG": r_gain, "rQ": r_quantize,
+            "W": enc_widen, "I": enc_interleave, "EQ": enc_quantize, "DI": dec_interleave, "DQ": dec_quantize,
+            "G0": lambda i: grad_matmul(i, 0), "G1": lambda i: grad_matmul(i, 1),
+            "m0": lambda i: grad_min(i, 0), "m1": lambda i: grad_min(i, 1), "b": exp_bias,
+            "x0": lambda i: exp_half(i, 0), "x1": lambda i: exp_half(i, 1), "xs": exp_sum, "c": coef_b,
+            "C": direction, "C2": lambda i: direction(i, 2),
+            "D0": lambda i: gained(i, 0, nc.gpsimd), "D1": lambda i: gained(i, 1, nc.gpsimd),
+            "V0": lambda i: gained(i, 0, nc.vector), "V1": lambda i: gained(i, 1, nc.vector),
+            "g0": lambda i: gap_sum(i, 0), "g1": lambda i: gap_sum(i, 1), "rl": gap_relu,
+            "T": dg_transpose, "T0": lambda i: dg_transpose(i, (0,)), "T1": lambda i: dg_transpose(i, (1,)),
+            "y": dg_copy, "y0": lambda i: dg_copy(i, (0,)), "y1": lambda i: dg_copy(i, (1,)),
+            "q": dg_quantize, "q0": lambda i: dg_quantize(i, (0,)), "q1": lambda i: dg_quantize(i, (1,)),
+            "E": e_matmul, "s": curvature, "r": gamma_a, "k": gamma_c,
+            "u": update, "u2": lambda i: update(i, 2),
+            "I128": lambda c: enc_interleave(c, 128),
+        }
+        done = set()
+        kept = set(TAIL)
+
+        def go(name, i):
+            if (name, i) not in done:
+                done.add((name, i))
+                ops[name](i)
+
+        for name, i in HEAD:
+            go(name, i)
+        for i in range(STEPS):
+            for name, off in LOOP:
+                t = i + off
+                if not 0 <= t < TILES:
+                    continue
+                if name in ("rT", "rG", "rQ"):
+                    if t % 2 == 0:
+                        go(name, t // 2)
+                elif (name, t) not in kept and not (
+                    t in SPECIAL and name in ("C", "D0", "D1", "T", "y", "q", "u")
+                ):
+                    go(name, t)
+        for name, i in TAIL:
+            go(name, i)

@@ -16,21 +16,27 @@ AX = mybir.AxisListType
 
 N, K, M = 1024, 1024, 512
 P = 128
+SLOTS = 4
 TILES = N // P
-HALF = 512
-PASSES = K // HALF
+PAIRS = TILES // 2
+HALF = P * SLOTS
+HALVES = K // HALF
 RADIUS = 64.0
+EPS = 1e-6
 
-FLOPS = 2 * 2 * N * K * M
+FLOPS = 2 * (2 * N * K * M)
 
 CHUNK = 256
 CHUNKS = K // CHUNK
-S_PLANES = (2, 3, 3, 3)
-HEAD = [("rT", 0), ("W", 1), ("W", 2), ("rG", 0), ("W", 3), ("W", 0), ("I128", 3), ("I", 2), ("I", 0), ("I", 1), ("rQ", 0), ("EQ", 0), ("EQ", 1), ("G0", 0), ("EQ", 3), ("EQ", 2), ("G1", 0), ("DI", 1), ("DQ", 1), ("m0", 0), ("rT", 1), ("DI", 0), ("m1", 0), ("b", 0), ("rT", 2), ("G0", 1), ("rG", 1), ("rG", 2), ("DQ", 0), ("G1", 1), ("x0", 0), ("x1", 0), ("xs", 0), ("rQ", 2), ("c", 0), ("rQ", 1)]
-LOOP = [("m0", 1), ("m1", 1), ("C", 0), ("b", 1), ("rQ", 3), ("q", -1), ("E", -1), ("x0", 1), ("x1", 1), ("D0", 0), ("G0", 2), ("xs", 1), ("G1", 2), ("s", -1), ("u", -3), ("g0", 0), ("g1", 0), ("r", -2), ("D1", 0), ("rG", 4), ("rT", 5), ("T", 0), ("rl", 0), ("c", 1), ("y", 0), ("k", -2)]
-TAIL = [("q", 5), ("k", 4), ("C2", 7), ("u", 4), ("E", 5), ("V0", 7), ("V1", 7), ("s", 5), ("r", 5), ("q", 6), ("k", 5), ("T0", 7), ("g0", 7), ("T1", 7), ("y0", 7), ("y1", 7), ("E", 6), ("u", 5), ("q0", 7), ("s", 6), ("q1", 7), ("E", 7), ("s", 7), ("g1", 7), ("r", 6), ("k", 6), ("u", 6), ("rl", 7), ("r", 7), ("k", 7), ("u2", 7)]
-STEPS = 7
-SPECIAL = (7,)
+WIDENED_ON_SCALAR = (3, 0, 2, 4)
+LAID_ON_SCALAR = (0, 64, 256, 0)
+
+
+def side_by_side(grouped, planes, first, last):
+    return (
+        grouped[:, first:last, :].rearrange("q (c i) t -> q c t i", i=4),
+        planes[:, :, first:last].rearrange("q t (c i) -> q c t i", i=4),
+    )
 
 
 def tile_smoothedfrankwolfesimplexcoding_kernel(tc, r, z, p, enc_bytes, enc_scale, g, dec, out):
@@ -38,11 +44,11 @@ def tile_smoothedfrankwolfesimplexcoding_kernel(tc, r, z, p, enc_bytes, enc_scal
     gap_factor = -1.0 / math.sqrt(M * K)
     mean_root = 1.0 / math.sqrt(M)
 
-    r_rows = r.rearrange("(q j) k -> q j k", j=TILES)
-    z_rows = z.rearrange("(q j) k -> q j k", j=TILES)
-    out_rows = out.rearrange("(q j) m -> q j m", j=TILES)
-    enc_rows = enc_bytes.rearrange("(q t) n -> q t n", t=4)
-    dec_rows = dec.rearrange("(h q t) m -> h q t m", q=P, t=4)
+    r_rows = r.rearrange("(q i) k -> q i k", i=TILES)
+    z_rows = z.rearrange("(q i) c -> q i c", i=TILES)
+    out_rows = out.rearrange("(q i) k -> q i k", i=TILES)
+    enc_rows = enc_bytes.rearrange("(q t) c -> q t c", t=SLOTS)
+    dec_rows = dec.rearrange("(h q t) k -> h q t k", q=P, t=SLOTS)
 
     with ExitStack() as ctx:
         keep = ctx.enter_context(tc.tile_pool(name="keep", bufs=1))
@@ -51,131 +57,125 @@ def tile_smoothedfrankwolfesimplexcoding_kernel(tc, r, z, p, enc_bytes, enc_scal
         psum = ctx.enter_context(tc.psum_pool(name="psum", bufs=2))
         ctx.enter_context(tc.manual_schedule())
 
-        scale_t = keep.tile([P, 4], F32, name="scale_t")
-        p_t = keep.tile([P, 4], BF16, name="p_t")
-        enc_raw = [keep.tile([P, 4, HALF], U8, name="enc_raw%d" % h) for h in range(2)]
-        r_t = [keep.tile([P, 2, M], BF16, name="r_t%d" % m) for m in range(TILES // 2)]
-        z_t = [keep.tile([P, K], BF16, name="z_t%d" % j) for j in range(TILES)]
+        scale_t = keep.tile([P, SLOTS], F32, name="scale_t")
+        p_t = keep.tile([P, SLOTS], BF16, name="p_t")
         g_t = keep.tile([P, K], BF16, name="g_t")
-        dec_raw = [keep.tile([P, 4, M], BF16, name="dec_raw%d" % h) for h in range(PASSES)]
+        byte_t = [keep.tile([P, SLOTS, HALF], U8, name="byte_t%d" % h) for h in range(HALVES)]
+        r_t = [keep.tile([P, 2, M], BF16, name="r_t%d" % m) for m in range(PAIRS)]
+        z_t = [keep.tile([P, K], BF16, name="z_t%d" % i) for i in range(TILES)]
+        dec_t = [keep.tile([P, SLOTS, M], BF16, name="dec_t%d" % h) for h in range(HALVES)]
 
-        nc.scalar.dma_start(out=scale_t[:], in_=enc_scale.rearrange("(q t) o -> q (t o)", t=4))
-        nc.scalar.dma_start(out=p_t[:], in_=p.rearrange("(q t) -> q t", t=4))
-        nc.sync.dma_start(out=enc_raw[0][:], in_=enc_rows[:, :, 0:HALF])
-        nc.sync.dma_start(out=r_t[0][:], in_=r_rows[:, 0:2, :])
-        nc.sync.dma_start(out=enc_raw[1][:], in_=enc_rows[:, :, HALF:K])
-        nc.sync.dma_start(out=dec_raw[0][:], in_=dec_rows[0])
-        nc.sync.dma_start(out=r_t[1][:], in_=r_rows[:, 2:4, :])
-        nc.sync.dma_start(out=z_t[0][:], in_=z_rows[:, 0, :])
-        nc.sync.dma_start(out=dec_raw[1][:], in_=dec_rows[1])
+        def load_r(m):
+            nc.sync.dma_start(out=r_t[m][:], in_=r_rows[:, 2 * m : 2 * m + 2, :])
+
+        def load_z(i):
+            nc.sync.dma_start(out=z_t[i][:], in_=z_rows[:, i, :])
+
+        nc.scalar.dma_start(out=scale_t[:], in_=enc_scale.rearrange("(q t) o -> q (t o)", t=SLOTS))
+        nc.scalar.dma_start(out=p_t[:], in_=p.rearrange("(q t) -> q t", t=SLOTS))
+        nc.sync.dma_start(out=byte_t[0][:], in_=enc_rows[:, :, 0:HALF])
+        load_r(0)
+        nc.sync.dma_start(out=byte_t[1][:], in_=enc_rows[:, :, HALF:K])
+        load_r(1)
+        nc.sync.dma_start(out=dec_t[0][:], in_=dec_rows[0])
+        load_r(2)
+        load_z(0)
+        nc.sync.dma_start(out=dec_t[1][:], in_=dec_rows[1])
         nc.sync.dma_start(out=g_t[:], in_=g.partition_broadcast(P))
-        nc.sync.dma_start(out=z_t[1][:], in_=z_rows[:, 1, :])
-        nc.sync.dma_start(out=r_t[2][:], in_=r_rows[:, 4:6, :])
-        nc.sync.dma_start(out=z_t[2][:], in_=z_rows[:, 2, :])
-        nc.sync.dma_start(out=r_t[3][:], in_=r_rows[:, 6:8, :])
-        for j in range(3, TILES):
-            nc.sync.dma_start(out=z_t[j][:], in_=z_rows[:, j, :])
+        load_z(1)
+        load_r(3)
+        for i in range(2, TILES):
+            load_z(i)
 
+        first_exp = keep.tile([P, 1], F32, name="first_exp")
+        nc.vector.memset(first_exp[:], 0.0)
+        nc.scalar.activation(out=first_exp[:], in_=first_exp[:], func=ACT.Exp)
         ident = keep.tile([P, P], F32, name="ident")
-        warm = keep.tile([P, 1], F32, name="warm")
-        nc.vector.memset(warm[:], 0.0)
-        nc.scalar.activation(out=warm[:], in_=warm[:], func=ACT.Exp)
         make_identity(nc, ident[:])
 
-        enc_plane = [keep.tile([P, 4, CHUNK], BF16, name="enc_plane%d" % c) for c in range(CHUNKS)]
-        enc_group = [keep.tile([P, CHUNK, 4], BF16, name="enc_group%d" % c, align_bytes=64) for c in range(CHUNKS)]
+        enc_plane = [keep.tile([P, SLOTS, CHUNK], BF16, name="enc_plane%d" % c) for c in range(CHUNKS)]
+        enc_group = [keep.tile([P, CHUNK, SLOTS], BF16, name="enc_group%d" % c, align_bytes=64) for c in range(CHUNKS)]
         enc_codes = keep.tile([P, K], U32, name="enc_codes", align_bytes=64)
         enc_scales = keep.tile([P, K], U8, name="enc_scales", align_bytes=64)
-        dec_group = [keep.tile([P, M, 4], BF16, name="dec_group%d" % h, align_bytes=64) for h in range(PASSES)]
-        dec_codes = keep.tile([P, PASSES, M], U32, name="dec_codes", align_bytes=64)
-        dec_scales = keep.tile([P, PASSES, M], U8, name="dec_scales", align_bytes=64)
-        rp_codes = [keep.tile([P, 2 * P], U32, name="rp_codes%d" % m, align_bytes=64) for m in range(TILES // 2)]
-        rp_scales = [keep.tile([P, 2 * P], U8, name="rp_scales%d" % m, align_bytes=64) for m in range(TILES // 2)]
+        dec_group = [keep.tile([P, M, SLOTS], BF16, name="dec_group%d" % h, align_bytes=64) for h in range(HALVES)]
+        dec_codes = keep.tile([P, HALVES, M], U32, name="dec_codes", align_bytes=64)
+        dec_scales = keep.tile([P, HALVES, M], U8, name="dec_scales", align_bytes=64)
 
         def enc_widen(c):
             first = c * CHUNK % HALF
-            for t in range(4):
-                src = enc_raw[c * CHUNK // HALF][:, t, first : first + CHUNK].bitcast(FP8)
+            for t in range(SLOTS):
+                src = byte_t[c * CHUNK // HALF][:, t, first : first + CHUNK].bitcast(FP8)
                 dst = enc_plane[c][:, t, :]
-                if t < S_PLANES[c]:
+                if t < WIDENED_ON_SCALAR[c]:
                     nc.scalar.activation(out=dst, in_=src, func=ACT.Copy, scale=scale_t[:, t : t + 1])
                 else:
                     nc.vector.tensor_scalar(
                         out=dst, in0=src, scalar1=scale_t[:, t : t + 1], scalar2=None, op0=ALU.mult
                     )
 
-        def enc_interleave(c, s=0):
-            n = CHUNK - s
-            nc.vector.tensor_copy(out=enc_group[c][:, 0:n, :], in_=enc_plane[c][:, :, 0:n].rearrange("q t n -> q n t"))
-            if s:
-                nc.scalar.copy(out=enc_group[c][:, n:CHUNK, :], in_=enc_plane[c][:, :, n:CHUNK].rearrange("q t n -> q n t"))
+        def enc_lay(c):
+            split = CHUNK - LAID_ON_SCALAR[c]
+            if split > 0:
+                dst, src = side_by_side(enc_group[c], enc_plane[c], 0, split)
+                nc.vector.tensor_copy(out=dst, in_=src)
+            if split < CHUNK:
+                dst, src = side_by_side(enc_group[c], enc_plane[c], split, CHUNK)
+                nc.scalar.copy(out=dst, in_=src)
 
         def enc_quantize(c):
             cols = slice(c * CHUNK, (c + 1) * CHUNK)
             nc.vector.quantize_mx(
                 out=enc_codes[:, cols].bitcast(FP8X4),
                 scales=enc_scales[:, cols],
-                in_=enc_group[c][:].rearrange("q n t -> q (n t)"),
+                in_=enc_group[c][:].rearrange("q c t -> q (c t)"),
             )
 
-        def dec_interleave(h):
-            nc.scalar.copy(out=dec_group[h][:], in_=dec_raw[h][:].rearrange("q t n -> q n t"))
+        def dec_lay(h, part):
+            dst, src = side_by_side(dec_group[h], dec_t[h], 256 * part, 256 * (part + 1))
+            nc.scalar.copy(out=dst, in_=src)
 
         def dec_quantize(h):
             nc.vector.quantize_mx(
                 out=dec_codes[:, h, :].bitcast(FP8X4),
                 scales=dec_scales[:, h, :],
-                in_=dec_group[h][:].rearrange("q n t -> q (n t)"),
+                in_=dec_group[h][:].rearrange("q k t -> q (k t)"),
             )
 
-        rt = {}
-        rp = {}
+        r_turned, rp, rp_codes, rp_scales = {}, {}, {}, {}
 
-        def r_transpose(m):
-            rt[m] = psum.tile([P, 2, 2 * P], F32, name="rt%d" % m, tag="turn")
+        def r_turn(m):
+            r_turned[m] = psum.tile([P, 2, 2 * P], F32, name="r_turned%d" % m, tag="turned")
             for j in range(2):
                 words = r_t[m][:, j, :].bitcast(F32)
                 for u in range(2):
-                    nc.tensor.transpose(rt[m][:, u, j * P : (j + 1) * P], words[:, u::2], ident[:])
+                    nc.tensor.transpose(r_turned[m][:, u, j * P : (j + 1) * P], words[:, u::2], ident[:])
 
         def r_gain(m):
-            rp[m] = work.tile([P, 2 * P, 4], BF16, name="rp%d" % m, tag="rp", align_bytes=64)
+            rp[m] = work.tile([P, 2 * P, SLOTS], BF16, name="rp%d" % m, tag="rp", align_bytes=64)
+            halves_of_words = r_turned[m][:].rearrange("q u n -> q (u n)").bitcast(BF16)
             nc.vector.tensor_tensor(
-                out=rp[m][:].rearrange("q i (u e) -> q i u e", u=2),
-                in0=rt[m][:].rearrange("q u i -> q (u i)").bitcast(BF16).rearrange("q (u i e) -> q i u e", u=2, e=2),
+                out=rp[m][:].rearrange("q n (u e) -> q n u e", u=2),
+                in0=halves_of_words.rearrange("q (u n e) -> q n u e", u=2, e=2),
                 in1=p_t[:].rearrange("q (u e) -> q u e", u=2).unsqueeze(1).to_broadcast([P, 2 * P, 2, 2]),
                 op=ALU.mult,
             )
 
         def r_quantize(m):
+            rp_codes[m] = keep.tile([P, 2 * P], U32, name="rp_codes%d" % m, align_bytes=64)
+            rp_scales[m] = keep.tile([P, 2 * P], U8, name="rp_scales%d" % m, align_bytes=64)
             nc.vector.quantize_mx(
                 out=rp_codes[m][:].bitcast(FP8X4),
                 scales=rp_scales[m][:],
-                in_=rp[m][:].rearrange("q i t -> q (i t)"),
+                in_=rp[m][:].rearrange("q n t -> q (n t)"),
             )
 
-        grad = {}
-        mins = {}
-        bias = {}
-        ex = {}
-        sums = {}
-        coef = {}
-        d = {}
-        dg = {}
-        gaps = {}
-        turned = {}
-        dgt = {}
-        dq = {}
-        e = {}
-        curv = {}
-        gamma = {}
-        step = {}
-        tot = {}
-        pos = {}
+        grad, lows, low_parts, bias, ex, sums, sum_parts, coef = {}, {}, {}, {}, {}, {}, {}, {}
+        d, dg, gaps, gap, dg_turned, dgt, dg_codes, dg_scales = {}, {}, {}, {}, {}, {}, {}, {}
+        e, mean_sq, curv, curv_inv, step = {}, {}, {}, {}, {}
 
-        def grad_matmul(i, h):
+        def grad_half(i, h):
             grad[i, h] = psum.tile([P, HALF], F32, name="grad%d_%d" % (i, h), tag="grad%d" % h)
-            rows = slice((i % 2) * P, (i % 2 + 1) * P)
+            rows = slice(i % 2 * P, (i % 2 + 1) * P)
             cols = slice(h * HALF, (h + 1) * HALF)
             nc.tensor.matmul_mx(
                 out=grad[i, h][:],
@@ -187,21 +187,31 @@ def tile_smoothedfrankwolfesimplexcoding_kernel(tc, r, z, p, enc_bytes, enc_scal
                 stop=True,
             )
 
-        def grad_min(i, h):
+        def grad_low(i, h):
             if h == 0:
-                mins[i] = stat.tile([P, 2], F32, name="mins%d" % i, tag="mins")
-            nc.vector.tensor_reduce(out=mins[i][:, h : h + 1], in_=grad[i, h][:], axis=AX.X, op=ALU.min)
+                lows[i] = stat.tile([P, HALVES], F32, name="lows%d" % i, tag="lows")
+            nc.vector.tensor_reduce(out=lows[i][:, h : h + 1], in_=grad[i, h][:], axis=AX.X, op=ALU.min)
 
-        def exp_bias(i):
+        def exp_bias_vector(i):
             bias[i] = stat.tile([P, 1], F32, name="bias%d" % i, tag="bias")
             nc.vector.tensor_scalar(
-                out=bias[i][:], in0=mins[i][:, 0:1], scalar1=mins[i][:, 1:2], scalar2=2.0, op0=ALU.min, op1=ALU.mult
+                out=bias[i][:], in0=lows[i][:, 0:1], scalar1=lows[i][:, 1:2], scalar2=2.0, op0=ALU.min, op1=ALU.mult
+            )
+
+        def exp_bias_scalar(i):
+            bias[i] = stat.tile([P, 1], F32, name="bias%d" % i, tag="bias")
+            low_parts[i] = stat.tile([P, 2], F32, name="low_parts%d" % i, tag="low_parts")
+            a, b = lows[i][:, 0:1], lows[i][:, 1:2]
+            nc.scalar.activation(out=low_parts[i][:, 0:1], in_=a, func=ACT.Copy, scale=2.0)
+            nc.scalar.activation(out=low_parts[i][:, 1:2], in_=b, func=ACT.Relu, scale=-1.0, bias=a)
+            nc.scalar.activation(
+                out=bias[i][:], in_=low_parts[i][:, 1:2], func=ACT.Identity, scale=-2.0, bias=low_parts[i][:, 0:1]
             )
 
         def exp_half(i, h):
             if h == 0:
                 ex[i] = work.tile([P, K], F32, name="ex%d" % i, tag="ex")
-                sums[i] = stat.tile([P, 2], F32, name="sums%d" % i, tag="sums")
+                sums[i] = stat.tile([P, HALVES], F32, name="sums%d" % i, tag="sums")
             nc.scalar.activation(
                 out=ex[i][:, h * HALF : (h + 1) * HALF],
                 in_=grad[i, h][:],
@@ -212,21 +222,21 @@ def tile_smoothedfrankwolfesimplexcoding_kernel(tc, r, z, p, enc_bytes, enc_scal
             )
 
         def exp_sum(i):
-            tot[i] = stat.tile([P, 2], F32, name="tot%d" % i, tag="tot")
-            nc.scalar.activation(out=tot[i][:, 0:1], in_=sums[i][:, 0:1], func=ACT.Copy, scale=1.0 / RADIUS)
+            sum_parts[i] = stat.tile([P, 2], F32, name="sum_parts%d" % i, tag="sum_parts")
+            half_sum, whole_sum = sum_parts[i][:, 0:1], sum_parts[i][:, 1:2]
+            nc.scalar.activation(out=half_sum, in_=sums[i][:, 0:1], func=ACT.Copy, scale=1.0 / RADIUS)
             nc.scalar.activation(
-                out=tot[i][:, 1:2], in_=sums[i][:, 1:2], func=ACT.Identity, scale=1.0 / RADIUS, bias=tot[i][:, 0:1]
+                out=whole_sum, in_=sums[i][:, 1:2], func=ACT.Identity, scale=1.0 / RADIUS, bias=half_sum
             )
 
-        def coef_b(i):
+        def exp_coef(i):
             coef[i] = stat.tile([P, 1], F32, name="coef%d" % i, tag="coef")
-            nc.vector.reciprocal(out=coef[i][:], in_=tot[i][:, 1:2])
+            nc.vector.reciprocal(out=coef[i][:], in_=sum_parts[i][:, 1:2])
 
-        def direction(i, parts=1):
+        def direction(i):
             d[i] = work.tile([P, K], F32, name="d%d" % i, tag="d")
-            w = K // parts
-            for h in range(parts):
-                cols = slice(h * w, (h + 1) * w)
+            for h in range(HALVES):
+                cols = slice(h * HALF, (h + 1) * HALF)
                 nc.vector.scalar_tensor_tensor(
                     out=d[i][:, cols],
                     in0=ex[i][:, cols],
@@ -236,18 +246,18 @@ def tile_smoothedfrankwolfesimplexcoding_kernel(tc, r, z, p, enc_bytes, enc_scal
                     op1=ALU.subtract,
                 )
 
-        def gained(i, h, engine):
+        def dg_half(i, h, engine):
             if h == 0:
                 dg[i] = work.tile([P, K], BF16, name="dg%d" % i, tag="dg")
             cols = slice(h * HALF, (h + 1) * HALF)
             engine.tensor_tensor(out=dg[i][:, cols], in0=d[i][:, cols], in1=g_t[:, cols], op=ALU.mult)
 
-        def gap_sum(i, h):
+        def gap_half(i, h):
             if h == 0:
-                gaps[i] = stat.tile([P, 2], F32, name="gaps%d" % i, tag="gaps")
-            junk = work.tile([P, HALF], F32, name="junk%d_%d" % (i, h), tag="junk")
+                gaps[i] = stat.tile([P, HALVES], F32, name="gaps%d" % i, tag="gaps")
+            products = work.tile([P, HALF], F32, name="products%d_%d" % (i, h), tag="products")
             nc.vector.scalar_tensor_tensor(
-                out=junk[:],
+                out=products[:],
                 in0=grad[i, h][:],
                 scalar=gap_factor,
                 in1=d[i][:, h * HALF : (h + 1) * HALF],
@@ -256,87 +266,76 @@ def tile_smoothedfrankwolfesimplexcoding_kernel(tc, r, z, p, enc_bytes, enc_scal
                 accum_out=gaps[i][:, h : h + 1],
             )
 
-        def dg_transpose(i, halves=(0, 1)):
-            if 0 in halves:
-                turned[i] = psum.tile([P, 2, 2, P], F32, name="turned%d" % i, tag="turn")
-            words = dg[i][:].bitcast(F32)
-            for h in halves:
-                for u in range(2):
-                    nc.tensor.transpose(turned[i][:, h, u, :], words[:, 256 * h + u : 256 * (h + 1) : 2], ident[:])
+        def gap_clip(i):
+            gap[i] = stat.tile([P, 1], F32, name="gap%d" % i, tag="gap")
+            nc.scalar.activation(out=gap[i][:], in_=gaps[i][:, 0:1], func=ACT.Relu, bias=gaps[i][:, 1:2])
 
-        def dg_copy(i, halves=(0, 1)):
-            if 0 in halves:
-                dgt[i] = work.tile([P, 2, P, 4], BF16, name="dgt%d" % i, tag="dgt", align_bytes=64)
-            h0, h1 = halves[0], halves[-1] + 1
+        def dg_turn(i, h):
+            if h == 0:
+                dg_turned[i] = psum.tile([P, HALVES, 2, P], F32, name="dg_turned%d" % i, tag="turned")
+            words = dg[i][:].bitcast(F32)
+            first, last = h * HALF // 2, (h + 1) * HALF // 2
+            for u in range(2):
+                nc.tensor.transpose(dg_turned[i][:, h, u, :], words[:, first + u : last : 2], ident[:])
+
+        def dg_copy(i, first_h, last_h):
+            if first_h == 0:
+                dgt[i] = work.tile([P, HALVES, P, SLOTS], BF16, name="dgt%d" % i, tag="dgt", align_bytes=64)
+            words = dgt[i][:].rearrange("q h n t -> q (h n t)").bitcast(F32)
             nc.scalar.copy(
-                out=dgt[i][:]
-                .rearrange("q h i t -> q (h i t)")
-                .bitcast(F32)
-                .rearrange("q (h i u) -> q h i u", h=2, u=2)[:, h0:h1],
-                in_=turned[i][:].rearrange("q h u i -> q h i u")[:, h0:h1],
+                out=words.rearrange("q (h n u) -> q h n u", h=HALVES, u=2)[:, first_h:last_h],
+                in_=dg_turned[i][:].rearrange("q h u n -> q h n u")[:, first_h:last_h],
             )
 
-        def dg_quantize(i, halves=(0, 1)):
-            if 0 in halves:
-                codes = work.tile([P, 2 * P], U32, name="dq_codes%d" % i, tag="dq_codes", align_bytes=64)
-                scales = work.tile([P, 2 * P], U8, name="dq_scales%d" % i, tag="dq_scales", align_bytes=64)
-                dq[i] = (codes, scales)
-            codes, scales = dq[i]
-            h0, h1 = halves[0], halves[-1] + 1
-            cols = slice(h0 * P, h1 * P)
+        def dg_quantize(i, first_h, last_h):
+            if first_h == 0:
+                dg_codes[i] = work.tile([P, HALVES * P], U32, name="dg_codes%d" % i, tag="dg_codes", align_bytes=64)
+                dg_scales[i] = work.tile([P, HALVES * P], U8, name="dg_scales%d" % i, tag="dg_scales", align_bytes=64)
+            cols = slice(first_h * P, last_h * P)
             nc.vector.quantize_mx(
-                out=codes[:, cols].bitcast(FP8X4),
-                scales=scales[:, cols],
-                in_=dgt[i][:].rearrange("q h i t -> q (h i t)")[:, h0 * 4 * P : h1 * 4 * P],
+                out=dg_codes[i][:, cols].bitcast(FP8X4),
+                scales=dg_scales[i][:, cols],
+                in_=dgt[i][:].rearrange("q h n t -> q (h n t)")[:, first_h * P * SLOTS : last_h * P * SLOTS],
             )
 
         def e_matmul(i):
-            bank = psum.tile([P, M], F32, name="e%d" % i, tag="e")
-            e[i] = bank
-            codes, scales = dq[i]
-            for h in range(PASSES):
+            e[i] = psum.tile([P, M], F32, name="e%d" % i, tag="e")
+            for h in range(HALVES):
+                rows = slice(h * P, (h + 1) * P)
                 nc.tensor.matmul_mx(
-                    out=bank[:],
-                    lhsT=codes[:, h * P : (h + 1) * P].bitcast(FP8X4),
-                    lhsT_scale=scales[:, h * P : (h + 1) * P],
+                    out=e[i][:],
+                    lhsT=dg_codes[i][:, rows].bitcast(FP8X4),
+                    lhsT_scale=dg_scales[i][:, rows],
                     rhs=dec_codes[:, h, :].bitcast(FP8X4),
                     rhs_scale=dec_scales[:, h, :],
                     start=(h == 0),
-                    stop=(h == PASSES - 1),
+                    stop=(h == HALVES - 1),
                 )
 
         def curvature(i):
-            curv[i] = stat.tile([P, 3], F32, name="curv%d" % i, tag="curv")
-            square = work.tile([P, M], F32, name="square%d" % i, tag="square")
+            mean_sq[i] = stat.tile([P, 1], F32, name="mean_sq%d" % i, tag="mean_sq")
+            curv[i] = stat.tile([P, 1], F32, name="curv%d" % i, tag="curv")
+            squares = work.tile([P, M], F32, name="squares%d" % i, tag="squares")
             nc.scalar.activation(
-                out=square[:], in_=e[i][:], func=ACT.Square, scale=mean_root, accum_out=curv[i][:, 0:1]
+                out=squares[:], in_=e[i][:], func=ACT.Square, scale=mean_root, accum_out=mean_sq[i][:]
             )
-            nc.scalar.activation(out=curv[i][:, 1:2], in_=curv[i][:, 0:1], func=ACT.Copy, bias=1e-6)
+            nc.scalar.activation(out=curv[i][:], in_=mean_sq[i][:], func=ACT.Copy, bias=EPS)
 
-        def gap_relu(i):
-            pos[i] = stat.tile([P, 1], F32, name="pos%d" % i, tag="pos")
-            nc.scalar.activation(out=pos[i][:], in_=gaps[i][:, 0:1], func=ACT.Relu, bias=gaps[i][:, 1:2])
+        def curv_invert(i):
+            curv_inv[i] = stat.tile([P, 1], F32, name="curv_inv%d" % i, tag="curv_inv")
+            nc.vector.reciprocal(out=curv_inv[i][:], in_=curv[i][:])
 
-        def gamma_a(i):
-            gamma[i] = stat.tile([P, 1], F32, name="gamma%d" % i, tag="gamma")
-            nc.vector.reciprocal(out=gamma[i][:], in_=curv[i][:, 1:2])
-
-        def gamma_c(i):
+        def step_size(i):
             step[i] = stat.tile([P, 1], F32, name="step%d" % i, tag="step")
             nc.vector.tensor_scalar(
-                out=step[i][:],
-                in0=pos[i][:],
-                scalar1=gamma[i][:],
-                scalar2=1.0,
-                op0=ALU.mult,
-                op1=ALU.min,
+                out=step[i][:], in0=gap[i][:], scalar1=curv_inv[i][:], scalar2=1.0, op0=ALU.mult, op1=ALU.min
             )
 
-        def update(i, parts=1):
+        def update(i, parts):
             res = work.tile([P, M], F32, name="res%d" % i, tag="res", bufs=4)
-            w = M // parts
-            for h in range(parts):
-                cols = slice(h * w, (h + 1) * w)
+            width = M // parts
+            for part in range(parts):
+                cols = slice(part * width, (part + 1) * width)
                 nc.vector.scalar_tensor_tensor(
                     out=res[:, cols],
                     in0=e[i][:, cols],
@@ -347,44 +346,149 @@ def tile_smoothedfrankwolfesimplexcoding_kernel(tc, r, z, p, enc_bytes, enc_scal
                 )
                 nc.sync.dma_start(out=out_rows[:, i, cols], in_=res[:, cols])
 
-        ops = {
-            "rT": r_transpose, "rG": r_gain, "rQ": r_quantize,
-            "W": enc_widen, "I": enc_interleave, "EQ": enc_quantize, "DI": dec_interleave, "DQ": dec_quantize,
-            "G0": lambda i: grad_matmul(i, 0), "G1": lambda i: grad_matmul(i, 1),
-            "m0": lambda i: grad_min(i, 0), "m1": lambda i: grad_min(i, 1), "b": exp_bias,
-            "x0": lambda i: exp_half(i, 0), "x1": lambda i: exp_half(i, 1), "xs": exp_sum, "c": coef_b,
-            "C": direction, "C2": lambda i: direction(i, 2),
-            "D0": lambda i: gained(i, 0, nc.gpsimd), "D1": lambda i: gained(i, 1, nc.gpsimd),
-            "V0": lambda i: gained(i, 0, nc.vector), "V1": lambda i: gained(i, 1, nc.vector),
-            "g0": lambda i: gap_sum(i, 0), "g1": lambda i: gap_sum(i, 1), "rl": gap_relu,
-            "T": dg_transpose, "T0": lambda i: dg_transpose(i, (0,)), "T1": lambda i: dg_transpose(i, (1,)),
-            "y": dg_copy, "y0": lambda i: dg_copy(i, (0,)), "y1": lambda i: dg_copy(i, (1,)),
-            "q": dg_quantize, "q0": lambda i: dg_quantize(i, (0,)), "q1": lambda i: dg_quantize(i, (1,)),
-            "E": e_matmul, "s": curvature, "r": gamma_a, "k": gamma_c,
-            "u": update, "u2": lambda i: update(i, 2),
-            "I128": lambda c: enc_interleave(c, 128),
-        }
-        done = set()
-        kept = set(TAIL)
+        r_turn(0)
+        for c in range(CHUNKS):
+            enc_widen(c)
+        enc_lay(1)
+        enc_lay(2)
+        enc_lay(0)
+        dec_lay(0, 1)
+        r_gain(0)
+        enc_quantize(0)
+        r_turn(1)
+        r_quantize(0)
+        enc_quantize(1)
+        enc_lay(3)
+        dec_lay(0, 0)
+        enc_quantize(2)
+        grad_half(0, 0)
+        enc_quantize(3)
+        grad_half(0, 1)
+        r_gain(1)
+        grad_low(0, 0)
+        grad_low(0, 1)
+        grad_half(1, 0)
+        exp_bias_vector(0)
+        r_turn(2)
+        exp_half(0, 0)
+        exp_half(0, 1)
+        exp_sum(0)
+        grad_half(1, 1)
+        grad_low(1, 0)
+        dec_quantize(0)
+        grad_low(1, 1)
+        r_quantize(1)
+        exp_bias_scalar(1)
+        exp_coef(0)
+        direction(0)
+        gap_half(0, 0)
+        r_gain(2)
+        dec_lay(1, 1)
+        gap_half(0, 1)
+        dg_half(0, 0, nc.gpsimd)
+        exp_half(1, 0)
+        dec_lay(1, 0)
+        exp_half(1, 1)
+        grad_half(2, 0)
+        grad_low(2, 0)
+        dec_quantize(1)
+        exp_sum(1)
+        dg_half(0, 1, nc.gpsimd)
+        grad_half(2, 1)
+        r_turn(3)
+        exp_coef(1)
 
-        def go(name, i):
-            if (name, i) not in done:
-                done.add((name, i))
-                ops[name](i)
+        for i in range(TILES - 3):
+            grad_low(i + 2, 1)
+            if i >= 2:
+                curv_invert(i - 2)
+            if i in (0, 2):
+                r_quantize(2 + i // 2)
+            for h in range(HALVES):
+                dg_turn(i, h)
+            if i >= 1:
+                gap_clip(i - 1)
+                dg_quantize(i - 1, 0, HALVES)
+            direction(i + 1)
+            exp_bias_scalar(i + 2)
+            exp_half(i + 2, 0)
+            if i >= 2:
+                step_size(i - 2)
+            exp_half(i + 2, 1)
+            gap_half(i + 1, 0)
+            gap_half(i + 1, 1)
+            dg_half(i + 1, 0, nc.gpsimd)
+            exp_sum(i + 2)
+            if i == 0:
+                r_gain(3)
+            if i >= 1:
+                e_matmul(i - 1)
+            grad_half(i + 3, 0)
+            exp_coef(i + 2)
+            if i >= 1:
+                curvature(i - 1)
+            grad_half(i + 3, 1)
+            if i >= 2:
+                update(i - 2, 1)
+            dg_half(i + 1, 1, nc.gpsimd)
+            dg_copy(i, 0, HALVES)
+            grad_low(i + 3, 0)
 
-        for name, i in HEAD:
-            go(name, i)
-        for i in range(STEPS):
-            for name, off in LOOP:
-                t = i + off
-                if not 0 <= t < TILES:
-                    continue
-                if name in ("rT", "rG", "rQ"):
-                    if t % 2 == 0:
-                        go(name, t // 2)
-                elif (name, t) not in kept and not (
-                    t in SPECIAL and name in ("C", "D0", "D1", "T", "y", "q", "u")
-                ):
-                    go(name, t)
-        for name, i in TAIL:
-            go(name, i)
+        curv_invert(3)
+        for h in range(HALVES):
+            dg_turn(5, h)
+        gap_clip(4)
+        dg_quantize(4, 0, HALVES)
+        step_size(3)
+        update(3, 1)
+        dg_copy(5, 0, HALVES)
+        gap_clip(5)
+        e_matmul(4)
+        grad_low(7, 1)
+        dg_quantize(5, 0, HALVES)
+        curvature(4)
+        exp_bias_scalar(7)
+        direction(6)
+        dg_half(6, 0, nc.gpsimd)
+        curv_invert(4)
+        gap_half(6, 0)
+        step_size(4)
+        gap_half(6, 1)
+        exp_half(7, 0)
+        exp_half(7, 1)
+        exp_sum(7)
+        e_matmul(5)
+        update(4, 1)
+        exp_coef(7)
+        curvature(5)
+        dg_half(6, 1, nc.gpsimd)
+        direction(7)
+        dg_half(7, 0, nc.vector)
+        for h in range(HALVES):
+            dg_turn(6, h)
+        dg_turn(7, 0)
+        dg_half(7, 1, nc.vector)
+        dg_copy(6, 0, HALVES)
+        curv_invert(5)
+        dg_quantize(6, 0, HALVES)
+        step_size(5)
+        dg_turn(7, 1)
+        dg_copy(7, 0, 1)
+        e_matmul(6)
+        dg_copy(7, 1, 2)
+        gap_clip(6)
+        curvature(6)
+        gap_half(7, 0)
+        update(5, 1)
+        dg_quantize(7, 0, 1)
+        dg_quantize(7, 1, 2)
+        gap_half(7, 1)
+        e_matmul(7)
+        curv_invert(6)
+        step_size(6)
+        curvature(7)
+        update(6, 1)
+        gap_clip(7)
+        curv_invert(7)
+        step_size(7)
+        update(7, 2)

import math
from contextlib import ExitStack

import concourse.mybir as mybir
from concourse.masks import make_identity

F32 = mybir.dt.float32
BF16 = mybir.dt.bfloat16
U32 = mybir.dt.uint32
U8 = mybir.dt.uint8
FP8 = mybir.dt.float8_e4m3fn
FP8X4 = mybir.dt.float8_e4m3fn_x4
ALU = mybir.AluOpType
ACT = mybir.ActivationFunctionType
AX = mybir.AxisListType

N, K, M = 1024, 1024, 512
P = 128
SLOTS = 4
TILES = N // P
PAIRS = TILES // 2
HALF = P * SLOTS
HALVES = K // HALF
RADIUS = 64.0
EPS = 1e-6

FLOPS = 2 * (2 * N * K * M)

CHUNK = 256
CHUNKS = K // CHUNK
WIDENED_ON_SCALAR = (3, 0, 2, 4)
LAID_ON_SCALAR = (0, 64, 256, 0)


def side_by_side(grouped, planes, first, last):
    return (
        grouped[:, first:last, :].rearrange("q (c i) t -> q c t i", i=4),
        planes[:, :, first:last].rearrange("q t (c i) -> q c t i", i=4),
    )


def tile_smoothedfrankwolfesimplexcoding_kernel(tc, r, z, p, enc_bytes, enc_scale, g, dec, out):
    nc = tc.nc
    gap_factor = -1.0 / math.sqrt(M * K)
    mean_root = 1.0 / math.sqrt(M)

    r_rows = r.rearrange("(q i) k -> q i k", i=TILES)
    z_rows = z.rearrange("(q i) c -> q i c", i=TILES)
    out_rows = out.rearrange("(q i) k -> q i k", i=TILES)
    enc_rows = enc_bytes.rearrange("(q t) c -> q t c", t=SLOTS)
    dec_rows = dec.rearrange("(h q t) k -> h q t k", q=P, t=SLOTS)

    with ExitStack() as ctx:
        keep = ctx.enter_context(tc.tile_pool(name="keep", bufs=1))
        work = ctx.enter_context(tc.tile_pool(name="work", bufs=2))
        stat = ctx.enter_context(tc.tile_pool(name="stat", bufs=6))
        psum = ctx.enter_context(tc.psum_pool(name="psum", bufs=2))
        ctx.enter_context(tc.manual_schedule())

        scale_t = keep.tile([P, SLOTS], F32, name="scale_t")
        p_t = keep.tile([P, SLOTS], BF16, name="p_t")
        g_t = keep.tile([P, K], BF16, name="g_t")
        byte_t = [keep.tile([P, SLOTS, HALF], U8, name="byte_t%d" % h) for h in range(HALVES)]
        r_t = [keep.tile([P, 2, M], BF16, name="r_t%d" % m) for m in range(PAIRS)]
        z_t = [keep.tile([P, K], BF16, name="z_t%d" % i) for i in range(TILES)]
        dec_t = [keep.tile([P, SLOTS, M], BF16, name="dec_t%d" % h) for h in range(HALVES)]

        def load_r(m):
            nc.sync.dma_start(out=r_t[m][:], in_=r_rows[:, 2 * m : 2 * m + 2, :])

        def load_z(i):
            nc.sync.dma_start(out=z_t[i][:], in_=z_rows[:, i, :])

        nc.scalar.dma_start(out=scale_t[:], in_=enc_scale.rearrange("(q t) o -> q (t o)", t=SLOTS))
        nc.scalar.dma_start(out=p_t[:], in_=p.rearrange("(q t) -> q t", t=SLOTS))
        nc.sync.dma_start(out=byte_t[0][:], in_=enc_rows[:, :, 0:HALF])
        load_r(0)
        nc.sync.dma_start(out=byte_t[1][:], in_=enc_rows[:, :, HALF:K])
        load_r(1)
        nc.sync.dma_start(out=dec_t[0][:], in_=dec_rows[0])
        load_r(2)
        load_z(0)
        nc.sync.dma_start(out=dec_t[1][:], in_=dec_rows[1])
        nc.sync.dma_start(out=g_t[:], in_=g.partition_broadcast(P))
        load_z(1)
        load_r(3)
        for i in range(2, TILES):
            load_z(i)

        first_exp = keep.tile([P, 1], F32, name="first_exp")
        nc.vector.memset(first_exp[:], 0.0)
        nc.scalar.activation(out=first_exp[:], in_=first_exp[:], func=ACT.Exp)
        ident = keep.tile([P, P], F32, name="ident")
        make_identity(nc, ident[:])

        enc_plane = [keep.tile([P, SLOTS, CHUNK], BF16, name="enc_plane%d" % c) for c in range(CHUNKS)]
        enc_group = [keep.tile([P, CHUNK, SLOTS], BF16, name="enc_group%d" % c, align_bytes=64) for c in range(CHUNKS)]
        enc_codes = keep.tile([P, K], U32, name="enc_codes", align_bytes=64)
        enc_scales = keep.tile([P, K], U8, name="enc_scales", align_bytes=64)
        dec_group = [keep.tile([P, M, SLOTS], BF16, name="dec_group%d" % h, align_bytes=64) for h in range(HALVES)]
        dec_codes = keep.tile([P, HALVES, M], U32, name="dec_codes", align_bytes=64)
        dec_scales = keep.tile([P, HALVES, M], U8, name="dec_scales", align_bytes=64)

        def enc_widen(c):
            first = c * CHUNK % HALF
            for t in range(SLOTS):
                src = byte_t[c * CHUNK // HALF][:, t, first : first + CHUNK].bitcast(FP8)
                dst = enc_plane[c][:, t, :]
                if t < WIDENED_ON_SCALAR[c]:
                    nc.scalar.activation(out=dst, in_=src, func=ACT.Copy, scale=scale_t[:, t : t + 1])
                else:
                    nc.vector.tensor_scalar(
                        out=dst, in0=src, scalar1=scale_t[:, t : t + 1], scalar2=None, op0=ALU.mult
                    )

        def enc_lay(c):
            split = CHUNK - LAID_ON_SCALAR[c]
            if split > 0:
                dst, src = side_by_side(enc_group[c], enc_plane[c], 0, split)
                nc.vector.tensor_copy(out=dst, in_=src)
            if split < CHUNK:
                dst, src = side_by_side(enc_group[c], enc_plane[c], split, CHUNK)
                nc.scalar.copy(out=dst, in_=src)

        def enc_quantize(c):
            cols = slice(c * CHUNK, (c + 1) * CHUNK)
            nc.vector.quantize_mx(
                out=enc_codes[:, cols].bitcast(FP8X4),
                scales=enc_scales[:, cols],
                in_=enc_group[c][:].rearrange("q c t -> q (c t)"),
            )

        def dec_lay(h, part):
            dst, src = side_by_side(dec_group[h], dec_t[h], 256 * part, 256 * (part + 1))
            nc.scalar.copy(out=dst, in_=src)

        def dec_quantize(h):
            nc.vector.quantize_mx(
                out=dec_codes[:, h, :].bitcast(FP8X4),
                scales=dec_scales[:, h, :],
                in_=dec_group[h][:].rearrange("q k t -> q (k t)"),
            )

        r_turned, rp, rp_codes, rp_scales = {}, {}, {}, {}

        def r_turn(m):
            r_turned[m] = psum.tile([P, 2, 2 * P], F32, name="r_turned%d" % m, tag="turned")
            for j in range(2):
                words = r_t[m][:, j, :].bitcast(F32)
                for u in range(2):
                    nc.tensor.transpose(r_turned[m][:, u, j * P : (j + 1) * P], words[:, u::2], ident[:])

        def r_gain(m):
            rp[m] = work.tile([P, 2 * P, SLOTS], BF16, name="rp%d" % m, tag="rp", align_bytes=64)
            halves_of_words = r_turned[m][:].rearrange("q u n -> q (u n)").bitcast(BF16)
            nc.vector.tensor_tensor(
                out=rp[m][:].rearrange("q n (u e) -> q n u e", u=2),
                in0=halves_of_words.rearrange("q (u n e) -> q n u e", u=2, e=2),
                in1=p_t[:].rearrange("q (u e) -> q u e", u=2).unsqueeze(1).to_broadcast([P, 2 * P, 2, 2]),
                op=ALU.mult,
            )

        def r_quantize(m):
            rp_codes[m] = keep.tile([P, 2 * P], U32, name="rp_codes%d" % m, align_bytes=64)
            rp_scales[m] = keep.tile([P, 2 * P], U8, name="rp_scales%d" % m, align_bytes=64)
            nc.vector.quantize_mx(
                out=rp_codes[m][:].bitcast(FP8X4),
                scales=rp_scales[m][:],
                in_=rp[m][:].rearrange("q n t -> q (n t)"),
            )

        grad, lows, low_parts, bias, ex, sums, sum_parts, coef = {}, {}, {}, {}, {}, {}, {}, {}
        d, dg, gaps, gap, dg_turned, dgt, dg_codes, dg_scales = {}, {}, {}, {}, {}, {}, {}, {}
        e, mean_sq, curv, curv_inv, step = {}, {}, {}, {}, {}

        def grad_half(i, h):
            grad[i, h] = psum.tile([P, HALF], F32, name="grad%d_%d" % (i, h), tag="grad%d" % h)
            rows = slice(i % 2 * P, (i % 2 + 1) * P)
            cols = slice(h * HALF, (h + 1) * HALF)
            nc.tensor.matmul_mx(
                out=grad[i, h][:],
                lhsT=rp_codes[i // 2][:, rows].bitcast(FP8X4),
                lhsT_scale=rp_scales[i // 2][:, rows],
                rhs=enc_codes[:, cols].bitcast(FP8X4),
                rhs_scale=enc_scales[:, cols],
                start=True,
                stop=True,
            )

        def grad_low(i, h):
            if h == 0:
                lows[i] = stat.tile([P, HALVES], F32, name="lows%d" % i, tag="lows")
            nc.vector.tensor_reduce(out=lows[i][:, h : h + 1], in_=grad[i, h][:], axis=AX.X, op=ALU.min)

        def exp_bias_vector(i):
            bias[i] = stat.tile([P, 1], F32, name="bias%d" % i, tag="bias")
            nc.vector.tensor_scalar(
                out=bias[i][:], in0=lows[i][:, 0:1], scalar1=lows[i][:, 1:2], scalar2=2.0, op0=ALU.min, op1=ALU.mult
            )

        def exp_bias_scalar(i):
            bias[i] = stat.tile([P, 1], F32, name="bias%d" % i, tag="bias")
            low_parts[i] = stat.tile([P, 2], F32, name="low_parts%d" % i, tag="low_parts")
            a, b = lows[i][:, 0:1], lows[i][:, 1:2]
            nc.scalar.activation(out=low_parts[i][:, 0:1], in_=a, func=ACT.Copy, scale=2.0)
            nc.scalar.activation(out=low_parts[i][:, 1:2], in_=b, func=ACT.Relu, scale=-1.0, bias=a)
            nc.scalar.activation(
                out=bias[i][:], in_=low_parts[i][:, 1:2], func=ACT.Identity, scale=-2.0, bias=low_parts[i][:, 0:1]
            )

        def exp_half(i, h):
            if h == 0:
                ex[i] = work.tile([P, K], F32, name="ex%d" % i, tag="ex")
                sums[i] = stat.tile([P, HALVES], F32, name="sums%d" % i, tag="sums")
            nc.scalar.activation(
                out=ex[i][:, h * HALF : (h + 1) * HALF],
                in_=grad[i, h][:],
                func=ACT.Exp,
                scale=-2.0,
                bias=bias[i][:],
                accum_out=sums[i][:, h : h + 1],
            )

        def exp_sum(i):
            sum_parts[i] = stat.tile([P, 2], F32, name="sum_parts%d" % i, tag="sum_parts")
            half_sum, whole_sum = sum_parts[i][:, 0:1], sum_parts[i][:, 1:2]
            nc.scalar.activation(out=half_sum, in_=sums[i][:, 0:1], func=ACT.Copy, scale=1.0 / RADIUS)
            nc.scalar.activation(
                out=whole_sum, in_=sums[i][:, 1:2], func=ACT.Identity, scale=1.0 / RADIUS, bias=half_sum
            )

        def exp_coef(i):
            coef[i] = stat.tile([P, 1], F32, name="coef%d" % i, tag="coef")
            nc.vector.reciprocal(out=coef[i][:], in_=sum_parts[i][:, 1:2])

        def direction(i):
            d[i] = work.tile([P, K], F32, name="d%d" % i, tag="d")
            for h in range(HALVES):
                cols = slice(h * HALF, (h + 1) * HALF)
                nc.vector.scalar_tensor_tensor(
                    out=d[i][:, cols],
                    in0=ex[i][:, cols],
                    scalar=coef[i][:],
                    in1=z_t[i][:, cols],
                    op0=ALU.mult,
                    op1=ALU.subtract,
                )

        def dg_half(i, h, engine):
            if h == 0:
                dg[i] = work.tile([P, K], BF16, name="dg%d" % i, tag="dg")
            cols = slice(h * HALF, (h + 1) * HALF)
            engine.tensor_tensor(out=dg[i][:, cols], in0=d[i][:, cols], in1=g_t[:, cols], op=ALU.mult)

        def gap_half(i, h):
            if h == 0:
                gaps[i] = stat.tile([P, HALVES], F32, name="gaps%d" % i, tag="gaps")
            products = work.tile([P, HALF], F32, name="products%d_%d" % (i, h), tag="products")
            nc.vector.scalar_tensor_tensor(
                out=products[:],
                in0=grad[i, h][:],
                scalar=gap_factor,
                in1=d[i][:, h * HALF : (h + 1) * HALF],
                op0=ALU.mult,
                op1=ALU.mult,
                accum_out=gaps[i][:, h : h + 1],
            )

        def gap_clip(i):
            gap[i] = stat.tile([P, 1], F32, name="gap%d" % i, tag="gap")
            nc.scalar.activation(out=gap[i][:], in_=gaps[i][:, 0:1], func=ACT.Relu, bias=gaps[i][:, 1:2])

        def dg_turn(i, h):
            if h == 0:
                dg_turned[i] = psum.tile([P, HALVES, 2, P], F32, name="dg_turned%d" % i, tag="turned")
            words = dg[i][:].bitcast(F32)
            first, last = h * HALF // 2, (h + 1) * HALF // 2
            for u in range(2):
                nc.tensor.transpose(dg_turned[i][:, h, u, :], words[:, first + u : last : 2], ident[:])

        def dg_copy(i, first_h, last_h):
            if first_h == 0:
                dgt[i] = work.tile([P, HALVES, P, SLOTS], BF16, name="dgt%d" % i, tag="dgt", align_bytes=64)
            words = dgt[i][:].rearrange("q h n t -> q (h n t)").bitcast(F32)
            nc.scalar.copy(
                out=words.rearrange("q (h n u) -> q h n u", h=HALVES, u=2)[:, first_h:last_h],
                in_=dg_turned[i][:].rearrange("q h u n -> q h n u")[:, first_h:last_h],
            )

        def dg_quantize(i, first_h, last_h):
            if first_h == 0:
                dg_codes[i] = work.tile([P, HALVES * P], U32, name="dg_codes%d" % i, tag="dg_codes", align_bytes=64)
                dg_scales[i] = work.tile([P, HALVES * P], U8, name="dg_scales%d" % i, tag="dg_scales", align_bytes=64)
            cols = slice(first_h * P, last_h * P)
            nc.vector.quantize_mx(
                out=dg_codes[i][:, cols].bitcast(FP8X4),
                scales=dg_scales[i][:, cols],
                in_=dgt[i][:].rearrange("q h n t -> q (h n t)")[:, first_h * P * SLOTS : last_h * P * SLOTS],
            )

        def e_matmul(i):
            e[i] = psum.tile([P, M], F32, name="e%d" % i, tag="e")
            for h in range(HALVES):
                rows = slice(h * P, (h + 1) * P)
                nc.tensor.matmul_mx(
                    out=e[i][:],
                    lhsT=dg_codes[i][:, rows].bitcast(FP8X4),
                    lhsT_scale=dg_scales[i][:, rows],
                    rhs=dec_codes[:, h, :].bitcast(FP8X4),
                    rhs_scale=dec_scales[:, h, :],
                    start=(h == 0),
                    stop=(h == HALVES - 1),
                )

        def curvature(i):
            mean_sq[i] = stat.tile([P, 1], F32, name="mean_sq%d" % i, tag="mean_sq")
            curv[i] = stat.tile([P, 1], F32, name="curv%d" % i, tag="curv")
            squares = work.tile([P, M], F32, name="squares%d" % i, tag="squares")
            nc.scalar.activation(
                out=squares[:], in_=e[i][:], func=ACT.Square, scale=mean_root, accum_out=mean_sq[i][:]
            )
            nc.scalar.activation(out=curv[i][:], in_=mean_sq[i][:], func=ACT.Copy, bias=EPS)

        def curv_invert(i):
            curv_inv[i] = stat.tile([P, 1], F32, name="curv_inv%d" % i, tag="curv_inv")
            nc.vector.reciprocal(out=curv_inv[i][:], in_=curv[i][:])

        def step_size(i):
            step[i] = stat.tile([P, 1], F32, name="step%d" % i, tag="step")
            nc.vector.tensor_scalar(
                out=step[i][:], in0=gap[i][:], scalar1=curv_inv[i][:], scalar2=1.0, op0=ALU.mult, op1=ALU.min
            )

        def update(i, parts):
            res = work.tile([P, M], F32, name="res%d" % i, tag="res", bufs=4)
            width = M // parts
            for part in range(parts):
                cols = slice(part * width, (part + 1) * width)
                nc.vector.scalar_tensor_tensor(
                    out=res[:, cols],
                    in0=e[i][:, cols],
                    scalar=step[i][:],
                    in1=r_t[i // 2][:, i % 2, cols],
                    op0=ALU.mult,
                    op1=ALU.add,
                )
                nc.sync.dma_start(out=out_rows[:, i, cols], in_=res[:, cols])

        r_turn(0)
        for c in range(CHUNKS):
            enc_widen(c)
        enc_lay(1)
        enc_lay(2)
        enc_lay(0)
        dec_lay(0, 1)
        r_gain(0)
        enc_quantize(0)
        r_turn(1)
        r_quantize(0)
        enc_quantize(1)
        enc_lay(3)
        dec_lay(0, 0)
        enc_quantize(2)
        grad_half(0, 0)
        enc_quantize(3)
        grad_half(0, 1)
        r_gain(1)
        grad_low(0, 0)
        grad_low(0, 1)
        grad_half(1, 0)
        exp_bias_vector(0)
        r_turn(2)
        exp_half(0, 0)
        exp_half(0, 1)
        exp_sum(0)
        grad_half(1, 1)
        grad_low(1, 0)
        dec_quantize(0)
        grad_low(1, 1)
        r_quantize(1)
        exp_bias_scalar(1)
        exp_coef(0)
        direction(0)
        gap_half(0, 0)
        r_gain(2)
        dec_lay(1, 1)
        gap_half(0, 1)
        dg_half(0, 0, nc.gpsimd)
        exp_half(1, 0)
        dec_lay(1, 0)
        exp_half(1, 1)
        grad_half(2, 0)
        grad_low(2, 0)
        dec_quantize(1)
        exp_sum(1)
        dg_half(0, 1, nc.gpsimd)
        grad_half(2, 1)
        r_turn(3)
        exp_coef(1)

        for i in range(TILES - 3):
            grad_low(i + 2, 1)
            if i >= 2:
                curv_invert(i - 2)
            if i in (0, 2):
                r_quantize(2 + i // 2)
            for h in range(HALVES):
                dg_turn(i, h)
            if i >= 1:
                gap_clip(i - 1)
                dg_quantize(i - 1, 0, HALVES)
            direction(i + 1)
            exp_bias_scalar(i + 2)
            exp_half(i + 2, 0)
            if i >= 2:
                step_size(i - 2)
            exp_half(i + 2, 1)
            gap_half(i + 1, 0)
            gap_half(i + 1, 1)
            dg_half(i + 1, 0, nc.gpsimd)
            exp_sum(i + 2)
            if i == 0:
                r_gain(3)
            if i >= 1:
                e_matmul(i - 1)
            grad_half(i + 3, 0)
            exp_coef(i + 2)
            if i >= 1:
                curvature(i - 1)
            grad_half(i + 3, 1)
            if i >= 2:
                update(i - 2, 1)
            dg_half(i + 1, 1, nc.gpsimd)
            dg_copy(i, 0, HALVES)
            grad_low(i + 3, 0)

        curv_invert(3)
        for h in range(HALVES):
            dg_turn(5, h)
        gap_clip(4)
        dg_quantize(4, 0, HALVES)
        step_size(3)
        update(3, 1)
        dg_copy(5, 0, HALVES)
        gap_clip(5)
        e_matmul(4)
        grad_low(7, 1)
        dg_quantize(5, 0, HALVES)
        curvature(4)
        exp_bias_scalar(7)
        direction(6)
        dg_half(6, 0, nc.gpsimd)
        curv_invert(4)
        gap_half(6, 0)
        step_size(4)
        gap_half(6, 1)
        exp_half(7, 0)
        exp_half(7, 1)
        exp_sum(7)
        e_matmul(5)
        update(4, 1)
        exp_coef(7)
        curvature(5)
        dg_half(6, 1, nc.gpsimd)
        direction(7)
        dg_half(7, 0, nc.vector)
        for h in range(HALVES):
            dg_turn(6, h)
        dg_turn(7, 0)
        dg_half(7, 1, nc.vector)
        dg_copy(6, 0, HALVES)
        curv_invert(5)
        dg_quantize(6, 0, HALVES)
        step_size(5)
        dg_turn(7, 1)
        dg_copy(7, 0, 1)
        e_matmul(6)
        dg_copy(7, 1, 2)
        gap_clip(6)
        curvature(6)
        gap_half(7, 0)
        update(5, 1)
        dg_quantize(7, 0, 1)
        dg_quantize(7, 1, 2)
        gap_half(7, 1)
        e_matmul(7)
        curv_invert(6)
        step_size(6)
        curvature(7)
        update(6, 1)
        gap_clip(7)
        curv_invert(7)
        step_size(7)
        update(7, 2)
